import numpy as np
import ml_dtypes


def mxq(x, axis, fmt="e4m3"):
    dtype, down = {"e4m3": (ml_dtypes.float8_e4m3fn, 7), "e5m2": (ml_dtypes.float8_e5m2, 14)}[fmt]
    v = np.moveaxis(np.asarray(x, np.float32).astype(ml_dtypes.bfloat16).astype(np.float64), axis, -1)
    blocks = v.reshape(v.shape[:-1] + (-1, 32))
    amax = np.abs(blocks).max(-1, keepdims=True)
    byte = np.maximum(np.where(amax > 0, np.frexp(amax)[1] - 1 + 127, 0) - down, 1)
    scale = np.exp2(byte - 127.0)
    codes = (blocks / scale).astype(np.float32).astype(dtype).astype(np.float64)
    return np.moveaxis((codes * scale).reshape(v.shape), -1, axis)


WIDE = False


def mx_kscale(k):
    if not WIDE:
        return np.ones(k)
    levels = np.array([18, -18])
    if k % 512:
        return np.exp2(np.random.permutation(np.resize(levels, k // 32))).repeat(32)
    a = np.empty((k // 512, 16))
    for p in range(k // 512):
        a[p, :8] = np.random.permutation(np.resize(levels, 8))
        for g in range(8):
            far = levels[np.abs(levels - a[p, g]) >= 10]
            a[p, g + 8] = far[np.random.randint(len(far))]
    return np.exp2(a.ravel()).repeat(32)


def f64(x):
    return np.asarray(x).astype(np.float64)


def striped(idx):
    return np.tile(np.asarray(idx).reshape(-1, 16).T, (8, 1)).astype(np.uint16)


def unstriped(offs):
    return offs[:16].T.reshape(-1).astype(np.int64)

def planes(y):
    n, m = y.shape
    v = y.astype(np.float32).astype(ml_dtypes.bfloat16).astype(np.float64).reshape(n // 32, 32, m)
    top = np.abs(v).max(1)
    byte = np.clip(np.where(top > 0, np.frexp(top)[1] - 1 + 127 - 7, 1), 1, 254)
    codes = (v * np.exp2(127.0 - byte)[:, None, :]).reshape(n, m).astype(np.float32).astype(ml_dtypes.float8_e4m3fn).view(np.uint8)
    words = codes.reshape(n // 512, 128, 4, m).transpose(0, 1, 3, 2)
    return np.ascontiguousarray(words), np.ascontiguousarray(byte.astype(np.uint8).reshape(n // 512, 16, m))


def setup_inputs():
    n = np.random.standard_normal
    uni = np.random.uniform
    q_ = np.random.permutation(512); par = np.empty(512, np.int64); par[q_[:256]] = q_[256:]; par[q_[256:]] = q_[:256]
    pr = par
    f_d = mx_kscale(512)
    f_m = mx_kscale(512)
    return {
        "w2": (n((512, 512)) / np.sqrt(512) * f_m[:, None] * f_d[None, :]).astype(np.float32),
        "dyT": (n((512, 512)) / f_m[:, None]).astype(np.float32),
        "w1": (n((512, 512)) / np.sqrt(512) / f_d[:, None]).astype(np.float32),
        "cs": np.tile(uni(-1.0, 1.0, 512), (128, 1)).astype(np.float32),
        "sn": np.tile(uni(-1.0, 1.0, 512), (128, 1)).astype(np.float32),
        "offs": striped(pr),
    }


def reference(w2, dyT, w1, cs, sn, offs):
    pr = unstriped(offs)
    u = mxq(f64(w2), 0, "e4m3").T @ mxq(f64(dyT), 0, "e5m2")
    up = u[:, pr]
    v = f64(cs)[:1] * u - f64(sn)[:1] * up
    out_0 = mxq(f64(w1), 0, "e4m3").T @ mxq(v, 0, "e5m2")
    return (out_0,) + planes(out_0)

@@ -1,0 +1,198 @@
+from contextlib import ExitStack
+
+import concourse.mybir as mybir
+from concourse.masks import make_identity
+
+F32 = mybir.dt.float32
+BF16 = mybir.dt.bfloat16
+I32 = mybir.dt.int32
+U32 = mybir.dt.uint32
+U16 = mybir.dt.uint16
+U8 = mybir.dt.uint8
+E4M3 = mybir.dt.float8_e4m3fn_x4
+E5M2 = mybir.dt.float8_e5m2_x4
+COPY = mybir.ActivationFunctionType.Copy
+MULT = mybir.AluOpType.mult
+SUBTRACT = mybir.AluOpType.subtract
+
+P = 128
+LANES = 4
+SIZE = 512
+SPARE = 16
+HALF = SIZE // 2
+DY_CHUNKS = ((0, 256), (256, 128), (384, 128))
+
+FLOPS = 2 * 2 * SIZE * SIZE * SIZE
+
+
+def tile_attend_gbutter_pl_kernel(tc, w2, dyT, w1, cs, sn, offs, out_0, out_1, out_2):
+    nc = tc.nc
+
+    def interleave(copy, dst, src):
+        copy(
+            out=dst.rearrange("p (c i) t -> p c t i", i=2),
+            in_=src.rearrange("p t (c i) -> p c t i", i=2),
+        )
+
+    def deal(copy, dst, src):
+        copy(
+            out=dst.rearrange("p t m j -> p m j t"),
+            in_=src.rearrange("p j (m t) -> p m j t", t=LANES),
+        )
+
+    def scalar_cast(out, in_):
+        nc.scalar.activation(out, in_, COPY)
+
+    def quantize(codes, scales, words, fmt):
+        nc.vector.quantize_mx(out=codes.bitcast(fmt), scales=scales, in_=words)
+
+    with ExitStack() as ctx:
+        sb = ctx.enter_context(tc.tile_pool(name="sb", bufs=1))
+        ps = ctx.enter_context(tc.psum_pool(name="ps", bufs=1))
+
+        def bank(index, name):
+            return ps.tile([P, SIZE], F32, name=name, tag="bank%d" % index)
+
+        offsets = sb.tile([P, SIZE // 16], U16, name="offsets")
+        identity = sb.tile([P, P], F32, name="identity")
+        make_identity(nc, identity[:])
+        u_sb = [sb.tile([P, SIZE + SPARE], F32, name="u%d" % t) for t in range(LANES)]
+        for t in range(LANES):
+            nc.gpsimd.memset(u_sb[t][:, SIZE:], 0.0)
+
+        w2_rows = w2.rearrange("(p j) d -> p j d", j=LANES)
+        dy_rows = dyT.rearrange("(p j) x -> p j x", j=LANES)
+        w1_rows = w1.rearrange("(p j) f -> p j f", j=LANES)
+        w2_raw = [sb.tile([P, LANES, HALF], F32, name="w2_raw%d" % h) for h in range(2)]
+        w1_raw = [sb.tile([P, LANES, HALF], F32, name="w1_raw%d" % h) for h in range(2)]
+        dy_raw = [sb.tile([P, LANES, n], F32, name="dy_raw%d" % x0) for x0, n in DY_CHUNKS]
+        sn_sb = sb.tile([P, SIZE], F32, name="sn_sb")
+        for h in range(2):
+            nc.sync.dma_start(out=w2_raw[h][:], in_=w2_rows[:, :, h * HALF : (h + 1) * HALF])
+        for raw, (x0, n) in zip(dy_raw, DY_CHUNKS):
+            nc.sync.dma_start(out=raw[:], in_=dy_rows[:, :, x0 : x0 + n])
+        nc.sync.dma_start(offsets[:], offs)
+        nc.sync.dma_start(out=sn_sb[:], in_=sn)
+        cs_cols = sb.tile([P, LANES], F32, name="cs_cols")
+        with nc.allow_non_contiguous_dma(reason="one factor a partition"):
+            nc.sync.dma_start(out=cs_cols[:], in_=cs[0, :].rearrange("(c p) -> p c", p=P))
+        for h in range(2):
+            nc.sync.dma_start(out=w1_raw[h][:], in_=w1_rows[:, :, h * HALF : (h + 1) * HALF])
+
+        w2_bf = sb.tile([P, LANES, P, LANES], BF16, name="w2_bf", align_bytes=64)
+        w2_codes = sb.tile([P, SIZE], U32, name="w2_codes", align_bytes=64)
+        w2_scales = sb.tile([P, SIZE], U8, name="w2_scales", align_bytes=64)
+        deal(scalar_cast, w2_bf[:, :, 0:64, :], w2_raw[0][:])
+        deal(nc.vector.tensor_copy, w2_bf[:, :, 64:128, :], w2_raw[1][:])
+        quantize(w2_codes[:], w2_scales[:], w2_bf[:].rearrange("p t m j -> p (t m j)"), E4M3)
+
+        dy_codes = sb.tile([P, SIZE], U32, name="dy_codes", align_bytes=64)
+        dy_scales = sb.tile([P, SIZE], U8, name="dy_scales", align_bytes=64)
+        dy_bf = [sb.tile([P, n, LANES], BF16, name="dy_bf%d" % x0, align_bytes=64) for x0, n in DY_CHUNKS]
+
+        def quantize_dy(k):
+            x0, n = DY_CHUNKS[k]
+            quantize(dy_codes[:, x0 : x0 + n], dy_scales[:, x0 : x0 + n], dy_bf[k][:].rearrange("p x t -> p (x t)"), E5M2)
+
+        interleave(nc.scalar.copy, dy_bf[0][:, 0:P, :], dy_raw[0][:, :, 0:P])
+        interleave(nc.vector.tensor_copy, dy_bf[0][:, P:, :], dy_raw[0][:, :, P:])
+        quantize_dy(0)
+        interleave(nc.scalar.copy, dy_bf[1][:], dy_raw[1][:])
+        interleave(nc.vector.tensor_copy, dy_bf[2][:], dy_raw[2][:])
+        quantize_dy(1)
+        quantize_dy(2)
+
+        def product(acc, lhs_codes, lhs_scales, rhs_codes, rhs_scales):
+            nc.tensor.matmul_mx(
+                out=acc[:],
+                lhsT=lhs_codes.bitcast(E4M3),
+                lhsT_scale=lhs_scales,
+                rhs=rhs_codes[:].bitcast(E5M2),
+                rhs_scale=rhs_scales[:],
+                start=True,
+                stop=True,
+            )
+
+        partner = sb.tile([P, LANES, SIZE], F32, name="partner", tag="partner", align_bytes=64)
+        uT_ps = [bank(4 + c, "uT_ps%d" % c) for c in range(4)]
+        for t in range(LANES):
+            u_ps = bank(t, "u_ps%d" % t)
+            product(u_ps, w2_codes[:, t * P : (t + 1) * P], w2_scales[:, t * P : (t + 1) * P], dy_codes, dy_scales)
+            nc.scalar.copy(out=u_sb[t][:, 0:SIZE], in_=u_ps[:])
+        for t in range(LANES):
+            nc.vector.tensor_tensor(partner[:, t, :], u_sb[t][:].indirect(offsets[:]), sn_sb[:], MULT)
+            for c in range(4):
+                nc.tensor.transpose(uT_ps[c][:, t * P : (t + 1) * P], u_sb[t][:, c * P : (c + 1) * P], identity[:])
+
+        own_ps = []
+        for c in range(4):
+            ownT = sb.tile([P, SIZE], F32, name="ownT%d" % c)
+            nc.scalar.activation(ownT[:], uT_ps[c][:], COPY, scale=cs_cols[:, c : c + 1])
+            own_ps.append(bank(c, "own_ps%d" % c))
+            for t in range(LANES):
+                nc.tensor.transpose(own_ps[c][:, t * P : (t + 1) * P], ownT[:, t * P : (t + 1) * P], identity[:])
+
+        w1_bf = sb.tile([P, LANES, P, LANES], BF16, name="w1_bf", align_bytes=64)
+        w1_scales = sb.tile([P, SIZE], U8, name="w1_scales", align_bytes=64)
+        for h in range(2):
+            deal(nc.scalar.copy, w1_bf[:, :, 64 * h : 64 * (h + 1), :], w1_raw[h][:])
+
+        v_codes = sb.tile([P, SIZE], U32, name="v_codes", align_bytes=64)
+        v_scales = sb.tile([P, SIZE], U8, name="v_scales", align_bytes=64)
+        v_bf = [sb.tile([P, P, LANES], BF16, name="v_bf%d" % c, tag="v_bf%d" % c, align_bytes=64) for c in range(4)]
+
+        def mix(c):
+            nc.vector.tensor_tensor(
+                v_bf[c][:].rearrange("p (c i) t -> p c t i", i=2),
+                own_ps[c][:].rearrange("p (t c i) -> p c t i", t=LANES, i=2),
+                partner[:, :, c * P : (c + 1) * P].rearrange("p t (c i) -> p c t i", i=2),
+                SUBTRACT,
+            )
+
+        def quantize_v(c):
+            cols = slice(c * P, (c + 1) * P)
+            quantize(v_codes[:, cols], v_scales[:, cols], v_bf[c][:].rearrange("p x t -> p (x t)"), E5M2)
+
+        mix(0)
+        for c in range(1, 4):
+            mix(c)
+            quantize_v(c - 1)
+        w1_first = sb.tile([P, P], U32, name="w1_first", tag="partner", align_bytes=64)
+        quantize(w1_first[:], w1_scales[:, 0:P], w1_bf[:, 0, :, :].rearrange("p m j -> p (m j)"), E4M3)
+        quantize_v(3)
+        w1_codes = [w1_first]
+        for t in range(1, LANES):
+            w1_codes.append(sb.tile([P, P], U32, name="w1_codes%d" % t, tag="v_bf%d" % t, align_bytes=64))
+            quantize(w1_codes[t][:], w1_scales[:, t * P : (t + 1) * P], w1_bf[:, t, :, :].rearrange("p m j -> p (m j)"), E4M3)
+
+        res = sb.tile([P, LANES, SIZE], F32, name="res")
+        out_rows = out_0.rearrange("(p t) x -> p t x", t=LANES)
+        for t in range(LANES):
+            acc = bank(4 + t, "acc%d" % t)
+            product(acc, w1_codes[t][:], w1_scales[:, t * P : (t + 1) * P], v_codes, v_scales)
+            if t == LANES - 1:
+                nc.scalar.copy(out=res[:, t, 0:HALF], in_=acc[:, 0:HALF])
+                nc.scalar.copy(out=res[:, t, HALF:], in_=acc[:, HALF:])
+            elif t == 1:
+                nc.scalar.copy(out=res[:, t, :], in_=acc[:])
+            else:
+                nc.vector.tensor_copy(out=res[:, t, :], in_=acc[:])
+            nc.sync.dma_start(out=out_rows[:, t, :], in_=res[:, t, :])
+
+        res_codes = sb.tile([P, SIZE], U32, name="res_codes", align_bytes=64)
+        res_scales = sb.tile([P, SIZE], U8, name="res_scales", align_bytes=64)
+        res_bf = [sb.tile([P, HALF, LANES], BF16, name="res_bf%d" % h, align_bytes=64) for h in range(2)]
+        out_words = out_1[0].rearrange("p x l -> p (x l)").bitcast(I32)
+        interleave(nc.vector.tensor_copy, res_bf[0][:], res[:, :, 0:HALF])
+        interleave(nc.vector.tensor_copy, res_bf[1][:, 0:64, :], res[:, :, HALF : HALF + 64])
+        interleave(nc.scalar.copy, res_bf[1][:, 64:, :], res[:, :, HALF + 64 : SIZE])
+        for h in range(2):
+            cols = slice(h * HALF, (h + 1) * HALF)
+            quantize(res_codes[:, cols], res_scales[:, cols], res_bf[h][:].rearrange("p x t -> p (x t)"), E4M3)
+            nc.sync.dma_start(out=out_words[:, cols], in_=res_codes[:, cols].bitcast(I32))
+        for q in range(4):
+            queue = nc.sync if q % 2 == 0 else nc.scalar
+            queue.dma_start(
+                out=out_2[0, 4 * q : 4 * q + 4, :].bitcast(I32),
+                in_=res_scales[32 * q : 32 * q + 4, :].bitcast(I32),
+            )

@@ -72,18 +72,19 @@ def tile_attend_gbutter_pl_kernel(tc, w2, dyT, w1, cs, sn, offs, out_0, out_1, o
         for raw, (x0, n) in zip(dy_raw, DY_CHUNKS):
             nc.sync.dma_start(out=raw[:], in_=dy_rows[:, :, x0 : x0 + n])
         nc.sync.dma_start(offsets[:], offs)
+        nc.sync.dma_start(out=w1_raw[0][:], in_=w1_rows[:, :, 0:HALF])
         nc.sync.dma_start(out=sn_sb[:], in_=sn)
         cs_cols = sb.tile([P, LANES], F32, name="cs_cols")
         with nc.allow_non_contiguous_dma(reason="one factor a partition"):
             nc.sync.dma_start(out=cs_cols[:], in_=cs[0, :].rearrange("(c p) -> p c", p=P))
-        for h in range(2):
-            nc.sync.dma_start(out=w1_raw[h][:], in_=w1_rows[:, :, h * HALF : (h + 1) * HALF])
+        nc.sync.dma_start(out=w1_raw[1][:], in_=w1_rows[:, :, HALF:])
 
         w2_bf = sb.tile([P, LANES, P, LANES], BF16, name="w2_bf", align_bytes=64)
         w2_codes = sb.tile([P, SIZE], U32, name="w2_codes", align_bytes=64)
         w2_scales = sb.tile([P, SIZE], U8, name="w2_scales", align_bytes=64)
-        deal(scalar_cast, w2_bf[:, :, 0:64, :], w2_raw[0][:])
-        deal(nc.vector.tensor_copy, w2_bf[:, :, 64:128, :], w2_raw[1][:])
+        deal(nc.vector.tensor_copy, w2_bf[:, :, 0:64, :], w2_raw[0][:])
+        deal(nc.vector.tensor_copy, w2_bf[:, :, 64:104, :], w2_raw[1][:, :, 0:160])
+        deal(scalar_cast, w2_bf[:, :, 104:, :], w2_raw[1][:, :, 160:])
         quantize(w2_codes[:], w2_scales[:], w2_bf[:].rearrange("p t m j -> p (t m j)"), E4M3)
 
         dy_codes = sb.tile([P, SIZE], U32, name="dy_codes", align_bytes=64)
@@ -120,11 +121,15 @@ def tile_attend_gbutter_pl_kernel(tc, w2, dyT, w1, cs, sn, offs, out_0, out_1, o
             product(u_ps, w2_codes[:, t * P : (t + 1) * P], w2_scales[:, t * P : (t + 1) * P], dy_codes, dy_scales)
             nc.scalar.copy(out=u_sb[t][:, 0:SIZE], in_=u_ps[:])
         for t in range(LANES):
-            nc.vector.tensor_tensor(partner[:, t, :], u_sb[t][:].indirect(offsets[:]), sn_sb[:], MULT)
-            for c in range(4):
-                nc.tensor.transpose(uT_ps[c][:, t * P : (t + 1) * P], u_sb[t][:, c * P : (c + 1) * P], identity[:])
+            pieces = ((0, HALF), (HALF, SIZE)) if t == LANES - 1 else ((0, SIZE),)
+            for x0, x1 in pieces:
+                looked_up = u_sb[t][:].indirect(offsets[:, x0 // 16 : x1 // 16])
+                nc.vector.tensor_tensor(partner[:, t, x0:x1], looked_up, sn_sb[:, x0:x1], MULT)
 
         own_ps = []
+        for c in range(4):
+            for t in range(LANES):
+                nc.tensor.transpose(uT_ps[c][:, t * P : (t + 1) * P], u_sb[t][:, c * P : (c + 1) * P], identity[:])
         for c in range(4):
             ownT = sb.tile([P, SIZE], F32, name="ownT%d" % c)
             nc.scalar.activation(ownT[:], uT_ps[c][:], COPY, scale=cs_cols[:, c : c + 1])
@@ -134,8 +139,9 @@ def tile_attend_gbutter_pl_kernel(tc, w2, dyT, w1, cs, sn, offs, out_0, out_1, o
 
         w1_bf = sb.tile([P, LANES, P, LANES], BF16, name="w1_bf", align_bytes=64)
         w1_scales = sb.tile([P, SIZE], U8, name="w1_scales", align_bytes=64)
-        for h in range(2):
-            deal(nc.scalar.copy, w1_bf[:, :, 64 * h : 64 * (h + 1), :], w1_raw[h][:])
+        deal(nc.vector.tensor_copy, w1_bf[:, :, 0:64, :], w1_raw[0][:])
+        deal(nc.scalar.copy, w1_bf[:, :, 64:96, :], w1_raw[1][:, :, 0:P])
+        deal(nc.scalar.copy, w1_bf[:, :, 96:, :], w1_raw[1][:, :, P:])
 
         v_codes = sb.tile([P, SIZE], U32, name="v_codes", align_bytes=64)
         v_scales = sb.tile([P, SIZE], U8, name="v_scales", align_bytes=64)
@@ -157,12 +163,12 @@ def tile_attend_gbutter_pl_kernel(tc, w2, dyT, w1, cs, sn, offs, out_0, out_1, o
         for c in range(1, 4):
             mix(c)
             quantize_v(c - 1)
-        w1_first = sb.tile([P, P], U32, name="w1_first", tag="partner", align_bytes=64)
+        w1_first = sb.tile([P, P], U32, name="w1_first", tag="v_bf1", align_bytes=64)
         quantize(w1_first[:], w1_scales[:, 0:P], w1_bf[:, 0, :, :].rearrange("p m j -> p (m j)"), E4M3)
         quantize_v(3)
         w1_codes = [w1_first]
         for t in range(1, LANES):
-            w1_codes.append(sb.tile([P, P], U32, name="w1_codes%d" % t, tag="v_bf%d" % t, align_bytes=64))
+            w1_codes.append(sb.tile([P, P], U32, name="w1_codes%d" % t, tag=("v_bf2", "partner", "v_bf3")[t - 1], align_bytes=64))
             quantize(w1_codes[t][:], w1_scales[:, t * P : (t + 1) * P], w1_bf[:, t, :, :].rearrange("p m j -> p (m j)"), E4M3)
 
         res = sb.tile([P, LANES, SIZE], F32, name="res")
@@ -177,7 +183,8 @@ def tile_attend_gbutter_pl_kernel(tc, w2, dyT, w1, cs, sn, offs, out_0, out_1, o
                 nc.scalar.copy(out=res[:, t, :], in_=acc[:])
             else:
                 nc.vector.tensor_copy(out=res[:, t, :], in_=acc[:])
-            nc.sync.dma_start(out=out_rows[:, t, :], in_=res[:, t, :])
+            if t % 2 == 1:
+                nc.sync.dma_start(out=out_rows[:, t - 1 : t + 1, :], in_=res[:, t - 1 : t + 1, :])
 
         res_codes = sb.tile([P, SIZE], U32, name="res_codes", align_bytes=64)
         res_scales = sb.tile([P, SIZE], U8, name="res_scales", align_bytes=64)

@@ -20,7 +20,8 @@ LANES = 4
 SIZE = 512
 SPARE = 16
 HALF = SIZE // 2
-DY_CHUNKS = ((0, 256), (256, 128), (384, 128))
+RUN = 4
+DY_SPLIT = 320
 
 FLOPS = 2 * 2 * SIZE * SIZE * SIZE
 
@@ -28,16 +29,10 @@ FLOPS = 2 * 2 * SIZE * SIZE * SIZE
 def tile_attend_gbutter_pl_kernel(tc, w2, dyT, w1, cs, sn, offs, out_0, out_1, out_2):
     nc = tc.nc
 
-    def interleave(copy, dst, src):
+    def interleave(copy, dst, src, run=2):
         copy(
-            out=dst.rearrange("p (c i) t -> p c t i", i=2),
-            in_=src.rearrange("p t (c i) -> p c t i", i=2),
-        )
-
-    def deal(copy, dst, src):
-        copy(
-            out=dst.rearrange("p t m j -> p m j t"),
-            in_=src.rearrange("p j (m t) -> p m j t", t=LANES),
+            out=dst.rearrange("p (c i) t -> p c t i", i=run),
+            in_=src.rearrange("p t (c i) -> p c t i", i=run),
         )
 
     def scalar_cast(out, in_):
@@ -60,48 +55,40 @@ def tile_attend_gbutter_pl_kernel(tc, w2, dyT, w1, cs, sn, offs, out_0, out_1, o
         for t in range(LANES):
             nc.gpsimd.memset(u_sb[t][:, SIZE:], 0.0)
 
-        w2_rows = w2.rearrange("(p j) d -> p j d", j=LANES)
-        dy_rows = dyT.rearrange("(p j) x -> p j x", j=LANES)
-        w1_rows = w1.rearrange("(p j) f -> p j f", j=LANES)
-        w2_raw = [sb.tile([P, LANES, HALF], F32, name="w2_raw%d" % h) for h in range(2)]
-        w1_raw = [sb.tile([P, LANES, HALF], F32, name="w1_raw%d" % h) for h in range(2)]
-        dy_raw = [sb.tile([P, LANES, n], F32, name="dy_raw%d" % x0) for x0, n in DY_CHUNKS]
+        w2_raw = sb.tile([P, LANES, SIZE], F32, name="w2_raw")
+        dy_raw = sb.tile([P, LANES, SIZE], F32, name="dy_raw")
+        w1_raw = sb.tile([P, LANES, SIZE], F32, name="w1_raw")
         sn_sb = sb.tile([P, SIZE], F32, name="sn_sb")
-        for h in range(2):
-            nc.sync.dma_start(out=w2_raw[h][:], in_=w2_rows[:, :, h * HALF : (h + 1) * HALF])
-        for raw, (x0, n) in zip(dy_raw, DY_CHUNKS):
-            nc.sync.dma_start(out=raw[:], in_=dy_rows[:, :, x0 : x0 + n])
+        nc.sync.dma_start(out=dy_raw[:], in_=dyT.rearrange("(p j) x -> p j x", j=LANES))
+        nc.sync.dma_start(out=w2_raw[:], in_=w2.rearrange("(p j) d -> p j d", j=LANES))
         nc.sync.dma_start(offsets[:], offs)
-        nc.sync.dma_start(out=w1_raw[0][:], in_=w1_rows[:, :, 0:HALF])
         nc.sync.dma_start(out=sn_sb[:], in_=sn)
-        cs_cols = sb.tile([P, LANES], F32, name="cs_cols")
+        cs_cols = sb.tile([P, LANES], F32, name="cs_cols", tag="late", align_bytes=64)
         with nc.allow_non_contiguous_dma(reason="one factor a partition"):
             nc.sync.dma_start(out=cs_cols[:], in_=cs[0, :].rearrange("(c p) -> p c", p=P))
-        nc.sync.dma_start(out=w1_raw[1][:], in_=w1_rows[:, :, HALF:])
+        w1_rows = w1.rearrange("(q t e) f -> e q t f", t=LANES, e=RUN)
+        for e in range(RUN):
+            nc.sync.dma_start(out=w1_raw[e:P:RUN, :, :], in_=w1_rows[e])
 
-        w2_bf = sb.tile([P, LANES, P, LANES], BF16, name="w2_bf", align_bytes=64)
+        dy_codes = sb.tile([P, SIZE], U32, name="dy_codes", tag="dy_codes", align_bytes=64)
+        dy_scales = sb.tile([P, SIZE], U8, name="dy_scales", align_bytes=64)
+        dy_bf = sb.tile([P, SIZE, LANES], BF16, name="dy_bf", align_bytes=64)
+        interleave(nc.vector.tensor_copy, dy_bf[:, 0:HALF, :], dy_raw[:, :, 0:HALF], 4)
+        interleave(nc.vector.tensor_copy, dy_bf[:, HALF:DY_SPLIT, :], dy_raw[:, :, HALF:DY_SPLIT], 4)
+        interleave(scalar_cast, dy_bf[:, DY_SPLIT:, :], dy_raw[:, :, DY_SPLIT:], 4)
+        for h in range(2):
+            cols = slice(h * HALF, (h + 1) * HALF)
+            quantize(dy_codes[:, cols], dy_scales[:, cols], dy_bf[:, cols, :].rearrange("p x t -> p (x t)"), E5M2)
+
         w2_codes = sb.tile([P, SIZE], U32, name="w2_codes", align_bytes=64)
         w2_scales = sb.tile([P, SIZE], U8, name="w2_scales", align_bytes=64)
-        deal(nc.vector.tensor_copy, w2_bf[:, :, 0:64, :], w2_raw[0][:])
-        deal(nc.vector.tensor_copy, w2_bf[:, :, 64:104, :], w2_raw[1][:, :, 0:160])
-        deal(scalar_cast, w2_bf[:, :, 104:, :], w2_raw[1][:, :, 160:])
-        quantize(w2_codes[:], w2_scales[:], w2_bf[:].rearrange("p t m j -> p (t m j)"), E4M3)
-
-        dy_codes = sb.tile([P, SIZE], U32, name="dy_codes", align_bytes=64)
-        dy_scales = sb.tile([P, SIZE], U8, name="dy_scales", align_bytes=64)
-        dy_bf = [sb.tile([P, n, LANES], BF16, name="dy_bf%d" % x0, align_bytes=64) for x0, n in DY_CHUNKS]
-
-        def quantize_dy(k):
-            x0, n = DY_CHUNKS[k]
-            quantize(dy_codes[:, x0 : x0 + n], dy_scales[:, x0 : x0 + n], dy_bf[k][:].rearrange("p x t -> p (x t)"), E5M2)
-
-        interleave(nc.scalar.copy, dy_bf[0][:, 0:P, :], dy_raw[0][:, :, 0:P])
-        interleave(nc.vector.tensor_copy, dy_bf[0][:, P:, :], dy_raw[0][:, :, P:])
-        quantize_dy(0)
-        interleave(nc.scalar.copy, dy_bf[1][:], dy_raw[1][:])
-        interleave(nc.vector.tensor_copy, dy_bf[2][:], dy_raw[2][:])
-        quantize_dy(1)
-        quantize_dy(2)
+        w2_runs = w2_raw[:].rearrange("p j (q t e) -> p t q j e", t=LANES, e=RUN)
+        for t in range(LANES):
+            w2_bf = sb.tile([P, P, LANES], BF16, name="w2_bf%d" % t, tag="w2_bf%d" % (0, 1, 0, 3)[t], align_bytes=64)
+            copy = nc.vector.tensor_copy if t % 2 == 0 else nc.scalar.copy
+            copy(out=w2_bf[:].rearrange("p (q e) j -> p q j e", e=RUN), in_=w2_runs[:, t])
+            cols = slice(t * P, (t + 1) * P)
+            quantize(w2_codes[:, cols], w2_scales[:, cols], w2_bf[:].rearrange("p m j -> p (m j)"), E4M3)
 
         def product(acc, lhs_codes, lhs_scales, rhs_codes, rhs_scales):
             nc.tensor.matmul_mx(
@@ -127,8 +114,8 @@ def tile_attend_gbutter_pl_kernel(tc, w2, dyT, w1, cs, sn, offs, out_0, out_1, o
                 nc.vector.tensor_tensor(partner[:, t, x0:x1], looked_up, sn_sb[:, x0:x1], MULT)
 
         own_ps = []
-        for c in range(4):
-            for t in range(LANES):
+        for t in range(LANES):
+            for c in range(4):
                 nc.tensor.transpose(uT_ps[c][:, t * P : (t + 1) * P], u_sb[t][:, c * P : (c + 1) * P], identity[:])
         for c in range(4):
             ownT = sb.tile([P, SIZE], F32, name="ownT%d" % c)
@@ -137,11 +124,13 @@ def tile_attend_gbutter_pl_kernel(tc, w2, dyT, w1, cs, sn, offs, out_0, out_1, o
             for t in range(LANES):
                 nc.tensor.transpose(own_ps[c][:, t * P : (t + 1) * P], ownT[:, t * P : (t + 1) * P], identity[:])
 
-        w1_bf = sb.tile([P, LANES, P, LANES], BF16, name="w1_bf", align_bytes=64)
+        w1_bf = [
+            sb.tile([P, 2, P, LANES], BF16, name="w1_bf%d" % h, tag=("dy_codes", "late")[h], align_bytes=64) for h in range(2)
+        ]
         w1_scales = sb.tile([P, SIZE], U8, name="w1_scales", align_bytes=64)
-        deal(nc.vector.tensor_copy, w1_bf[:, :, 0:64, :], w1_raw[0][:])
-        deal(nc.scalar.copy, w1_bf[:, :, 64:96, :], w1_raw[1][:, :, 0:P])
-        deal(nc.scalar.copy, w1_bf[:, :, 96:, :], w1_raw[1][:, :, P:])
+        w1_pairs = w1_raw[:].rearrange("p j (m h t) -> p h m j t", h=2, t=2)
+        for h in range(2):
+            nc.scalar.copy(out=w1_bf[h][:].rearrange("p t m j -> p m j t"), in_=w1_pairs[:, h])
 
         v_codes = sb.tile([P, SIZE], U32, name="v_codes", align_bytes=64)
         v_scales = sb.tile([P, SIZE], U8, name="v_scales", align_bytes=64)
@@ -164,12 +153,12 @@ def tile_attend_gbutter_pl_kernel(tc, w2, dyT, w1, cs, sn, offs, out_0, out_1, o
             mix(c)
             quantize_v(c - 1)
         w1_first = sb.tile([P, P], U32, name="w1_first", tag="v_bf1", align_bytes=64)
-        quantize(w1_first[:], w1_scales[:, 0:P], w1_bf[:, 0, :, :].rearrange("p m j -> p (m j)"), E4M3)
+        quantize(w1_first[:], w1_scales[:, 0:P], w1_bf[0][:, 0, :, :].rearrange("p m j -> p (m j)"), E4M3)
         quantize_v(3)
         w1_codes = [w1_first]
         for t in range(1, LANES):
             w1_codes.append(sb.tile([P, P], U32, name="w1_codes%d" % t, tag=("v_bf2", "partner", "v_bf3")[t - 1], align_bytes=64))
-            quantize(w1_codes[t][:], w1_scales[:, t * P : (t + 1) * P], w1_bf[:, t, :, :].rearrange("p m j -> p (m j)"), E4M3)
+            quantize(w1_codes[t][:], w1_scales[:, t * P : (t + 1) * P], w1_bf[t // 2][:, t % 2, :, :].rearrange("p m j -> p (m j)"), E4M3)
 
         res = sb.tile([P, LANES, SIZE], F32, name="res")
         out_rows = out_0.rearrange("(p t) x -> p t x", t=LANES)

@@ -90,12 +90,12 @@ def tile_attend_gbutter_pl_kernel(tc, w2, dyT, w1, cs, sn, offs, out_0, out_1, o
             cols = slice(t * P, (t + 1) * P)
             quantize(w2_codes[:, cols], w2_scales[:, cols], w2_bf[:].rearrange("p m j -> p (m j)"), E4M3)
 
-        def product(acc, lhs_codes, lhs_scales, rhs_codes, rhs_scales):
+        def product(acc, lhs_codes, lhs_scales, rhs_codes, rhs_scales, lhs_fmt=E4M3, rhs_fmt=E5M2):
             nc.tensor.matmul_mx(
                 out=acc[:],
-                lhsT=lhs_codes.bitcast(E4M3),
+                lhsT=lhs_codes.bitcast(lhs_fmt),
                 lhsT_scale=lhs_scales,
-                rhs=rhs_codes[:].bitcast(E5M2),
+                rhs=rhs_codes[:].bitcast(rhs_fmt),
                 rhs_scale=rhs_scales[:],
                 start=True,
                 stop=True,
@@ -107,25 +107,29 @@ def tile_attend_gbutter_pl_kernel(tc, w2, dyT, w1, cs, sn, offs, out_0, out_1, o
             u_ps = bank(t, "u_ps%d" % t)
             product(u_ps, w2_codes[:, t * P : (t + 1) * P], w2_scales[:, t * P : (t + 1) * P], dy_codes, dy_scales)
             nc.scalar.copy(out=u_sb[t][:, 0:SIZE], in_=u_ps[:])
+        for c in (3, 0):
+            product(uT_ps[c], dy_codes[:, c * P : (c + 1) * P], dy_scales[:, c * P : (c + 1) * P], w2_codes, w2_scales, E5M2, E4M3)
         for t in range(LANES):
             pieces = ((0, HALF), (HALF, SIZE)) if t == LANES - 1 else ((0, SIZE),)
             for x0, x1 in pieces:
                 looked_up = u_sb[t][:].indirect(offsets[:, x0 // 16 : x1 // 16])
                 nc.vector.tensor_tensor(partner[:, t, x0:x1], looked_up, sn_sb[:, x0:x1], MULT)
 
-        own_ps = []
+        own_ps = [None] * 4
         for t in range(LANES):
-            for c in range(4):
+            for c in (1, 2):
                 nc.tensor.transpose(uT_ps[c][:, t * P : (t + 1) * P], u_sb[t][:, c * P : (c + 1) * P], identity[:])
-        for c in range(4):
-            ownT = sb.tile([P, SIZE], F32, name="ownT%d" % c)
+        own_last = sb.tile([P, P, LANES], F32, name="own_last")
+        for c in (3, 0, 1, 2):
+            ownT = sb.tile([P, SIZE], F32, name="ownT%d" % c, tag="ownT%d" % c, align_bytes=64)
             nc.scalar.activation(ownT[:], uT_ps[c][:], COPY, scale=cs_cols[:, c : c + 1])
-            own_ps.append(bank(c, "own_ps%d" % c))
+            own_ps[c] = bank(c, "own_ps%d" % c)
             for t in range(LANES):
                 nc.tensor.transpose(own_ps[c][:, t * P : (t + 1) * P], ownT[:, t * P : (t + 1) * P], identity[:])
 
+        nc.scalar.copy(out=own_last[:], in_=own_ps[3][:].rearrange("p (t x) -> p x t", t=LANES))
         w1_bf = [
-            sb.tile([P, 2, P, LANES], BF16, name="w1_bf%d" % h, tag=("dy_codes", "late")[h], align_bytes=64) for h in range(2)
+            sb.tile([P, 2, P, LANES], BF16, name="w1_bf%d" % h, tag=("ownT1", "late")[h], align_bytes=64) for h in range(2)
         ]
         w1_scales = sb.tile([P, SIZE], U8, name="w1_scales", align_bytes=64)
         w1_pairs = w1_raw[:].rearrange("p j (m h t) -> p h m j t", h=2, t=2)
@@ -148,10 +152,11 @@ def tile_attend_gbutter_pl_kernel(tc, w2, dyT, w1, cs, sn, offs, out_0, out_1, o
             cols = slice(c * P, (c + 1) * P)
             quantize(v_codes[:, cols], v_scales[:, cols], v_bf[c][:].rearrange("p x t -> p (x t)"), E5M2)
 
-        mix(0)
-        for c in range(1, 4):
+        nc.gpsimd.tensor_tensor(v_bf[3][:], own_last[:], partner[:, :, 3 * P :].rearrange("p t x -> p x t"), SUBTRACT)
+        for c in range(3):
             mix(c)
-            quantize_v(c - 1)
+        for c in range(3):
+            quantize_v(c)
         w1_first = sb.tile([P, P], U32, name="w1_first", tag="v_bf1", align_bytes=64)
         quantize(w1_first[:], w1_scales[:, 0:P], w1_bf[0][:, 0, :, :].rearrange("p m j -> p (m j)"), E4M3)
         quantize_v(3)
@@ -172,8 +177,9 @@ def tile_attend_gbutter_pl_kernel(tc, w2, dyT, w1, cs, sn, offs, out_0, out_1, o
                 nc.scalar.copy(out=res[:, t, :], in_=acc[:])
             else:
                 nc.vector.tensor_copy(out=res[:, t, :], in_=acc[:])
-            if t % 2 == 1:
-                nc.sync.dma_start(out=out_rows[:, t - 1 : t + 1, :], in_=res[:, t - 1 : t + 1, :])
+            if t >= 1:
+                first = 0 if t == 1 else t
+                nc.sync.dma_start(out=out_rows[:, first : t + 1, :], in_=res[:, first : t + 1, :])
 
         res_codes = sb.tile([P, SIZE], U32, name="res_codes", align_bytes=64)
         res_scales = sb.tile([P, SIZE], U8, name="res_scales", align_bytes=64)

@@ -22,6 +22,8 @@ SPARE = 16
 HALF = SIZE // 2
 RUN = 4
 DY_SPLIT = 320
+W2_SPLIT = 20
+RES_SPLIT = 128
 
 FLOPS = 2 * 2 * SIZE * SIZE * SIZE
 
@@ -85,17 +87,22 @@ def tile_attend_gbutter_pl_kernel(tc, w2, dyT, w1, cs, sn, offs, out_0, out_1, o
         w2_runs = w2_raw[:].rearrange("p j (q t e) -> p t q j e", t=LANES, e=RUN)
         for t in range(LANES):
             w2_bf = sb.tile([P, P, LANES], BF16, name="w2_bf%d" % t, tag="w2_bf%d" % (0, 1, 0, 3)[t], align_bytes=64)
-            copy = nc.vector.tensor_copy if t % 2 == 0 else nc.scalar.copy
-            copy(out=w2_bf[:].rearrange("p (q e) j -> p q j e", e=RUN), in_=w2_runs[:, t])
+            cast = w2_bf[:].rearrange("p (q e) j -> p q j e", e=RUN)
+            if t == 0:
+                nc.vector.tensor_copy(out=cast[:, 0:W2_SPLIT], in_=w2_runs[:, t, 0:W2_SPLIT])
+                nc.scalar.copy(out=cast[:, W2_SPLIT:], in_=w2_runs[:, t, W2_SPLIT:])
+            else:
+                copy = nc.vector.tensor_copy if t == 2 else nc.scalar.copy
+                copy(out=cast, in_=w2_runs[:, t])
             cols = slice(t * P, (t + 1) * P)
             quantize(w2_codes[:, cols], w2_scales[:, cols], w2_bf[:].rearrange("p m j -> p (m j)"), E4M3)
 
-        def product(acc, lhs_codes, lhs_scales, rhs_codes, rhs_scales, lhs_fmt=E4M3, rhs_fmt=E5M2):
+        def product(acc, lhs_codes, lhs_scales, rhs_codes, rhs_scales):
             nc.tensor.matmul_mx(
                 out=acc[:],
-                lhsT=lhs_codes.bitcast(lhs_fmt),
+                lhsT=lhs_codes.bitcast(E4M3),
                 lhsT_scale=lhs_scales,
-                rhs=rhs_codes[:].bitcast(rhs_fmt),
+                rhs=rhs_codes[:].bitcast(E5M2),
                 rhs_scale=rhs_scales[:],
                 start=True,
                 stop=True,
@@ -107,8 +114,6 @@ def tile_attend_gbutter_pl_kernel(tc, w2, dyT, w1, cs, sn, offs, out_0, out_1, o
             u_ps = bank(t, "u_ps%d" % t)
             product(u_ps, w2_codes[:, t * P : (t + 1) * P], w2_scales[:, t * P : (t + 1) * P], dy_codes, dy_scales)
             nc.scalar.copy(out=u_sb[t][:, 0:SIZE], in_=u_ps[:])
-        for c in (3, 0):
-            product(uT_ps[c], dy_codes[:, c * P : (c + 1) * P], dy_scales[:, c * P : (c + 1) * P], w2_codes, w2_scales, E5M2, E4M3)
         for t in range(LANES):
             pieces = ((0, HALF), (HALF, SIZE)) if t == LANES - 1 else ((0, SIZE),)
             for x0, x1 in pieces:
@@ -116,18 +121,19 @@ def tile_attend_gbutter_pl_kernel(tc, w2, dyT, w1, cs, sn, offs, out_0, out_1, o
                 nc.vector.tensor_tensor(partner[:, t, x0:x1], looked_up, sn_sb[:, x0:x1], MULT)
 
         own_ps = [None] * 4
-        for t in range(LANES):
-            for c in (1, 2):
+        for c in (3, 0, 1, 2):
+            for t in range(LANES):
                 nc.tensor.transpose(uT_ps[c][:, t * P : (t + 1) * P], u_sb[t][:, c * P : (c + 1) * P], identity[:])
         own_last = sb.tile([P, P, LANES], F32, name="own_last")
         for c in (3, 0, 1, 2):
+            if c == 2:
+                nc.scalar.copy(out=own_last[:], in_=own_ps[3][:].rearrange("p (t x) -> p x t", t=LANES))
             ownT = sb.tile([P, SIZE], F32, name="ownT%d" % c, tag="ownT%d" % c, align_bytes=64)
             nc.scalar.activation(ownT[:], uT_ps[c][:], COPY, scale=cs_cols[:, c : c + 1])
             own_ps[c] = bank(c, "own_ps%d" % c)
             for t in range(LANES):
                 nc.tensor.transpose(own_ps[c][:, t * P : (t + 1) * P], ownT[:, t * P : (t + 1) * P], identity[:])
 
-        nc.scalar.copy(out=own_last[:], in_=own_ps[3][:].rearrange("p (t x) -> p x t", t=LANES))
         w1_bf = [
             sb.tile([P, 2, P, LANES], BF16, name="w1_bf%d" % h, tag=("ownT1", "late")[h], align_bytes=64) for h in range(2)
         ]
@@ -155,6 +161,9 @@ def tile_attend_gbutter_pl_kernel(tc, w2, dyT, w1, cs, sn, offs, out_0, out_1, o
         nc.gpsimd.tensor_tensor(v_bf[3][:], own_last[:], partner[:, :, 3 * P :].rearrange("p t x -> p x t"), SUBTRACT)
         for c in range(3):
             mix(c)
+        warm = bank(1, "warm")
+        for t in range(2):
+            product(warm, w2_codes[:, t * P : (t + 1) * P], w2_scales[:, t * P : (t + 1) * P], dy_codes, dy_scales)
         for c in range(3):
             quantize_v(c)
         w1_first = sb.tile([P, P], U32, name="w1_first", tag="v_bf1", align_bytes=64)
@@ -186,8 +195,8 @@ def tile_attend_gbutter_pl_kernel(tc, w2, dyT, w1, cs, sn, offs, out_0, out_1, o
         res_bf = [sb.tile([P, HALF, LANES], BF16, name="res_bf%d" % h, align_bytes=64) for h in range(2)]
         out_words = out_1[0].rearrange("p x l -> p (x l)").bitcast(I32)
         interleave(nc.vector.tensor_copy, res_bf[0][:], res[:, :, 0:HALF])
-        interleave(nc.vector.tensor_copy, res_bf[1][:, 0:64, :], res[:, :, HALF : HALF + 64])
-        interleave(nc.scalar.copy, res_bf[1][:, 64:, :], res[:, :, HALF + 64 : SIZE])
+        interleave(nc.vector.tensor_copy, res_bf[1][:, 0:RES_SPLIT, :], res[:, :, HALF : HALF + RES_SPLIT])
+        interleave(nc.scalar.copy, res_bf[1][:, RES_SPLIT:, :], res[:, :, HALF + RES_SPLIT : SIZE])
         for h in range(2):
             cols = slice(h * HALF, (h + 1) * HALF)
             quantize(res_codes[:, cols], res_scales[:, cols], res_bf[h][:].rearrange("p x t -> p (x t)"), E4M3)

@@ -59,18 +59,23 @@ def tile_attend_gbutter_pl_kernel(tc, w2, dyT, w1, cs, sn, offs, out_0, out_1, o
 
         w2_raw = sb.tile([P, LANES, SIZE], F32, name="w2_raw")
         dy_raw = sb.tile([P, LANES, SIZE], F32, name="dy_raw")
-        w1_raw = sb.tile([P, LANES, SIZE], F32, name="w1_raw")
+        w1_raw = [sb.tile([P, LANES, HALF], F32, name="w1_raw%d" % h) for h in range(2)]
+        w1_rows = w1.rearrange("(q t e) f -> e q t f", t=LANES, e=RUN)
+
+        def load_w1(h):
+            for e in range(RUN):
+                nc.sync.dma_start(out=w1_raw[h][e:P:RUN, :, :], in_=w1_rows[e][:, :, h * HALF : (h + 1) * HALF])
+
         sn_sb = sb.tile([P, SIZE], F32, name="sn_sb")
         nc.sync.dma_start(out=dy_raw[:], in_=dyT.rearrange("(p j) x -> p j x", j=LANES))
         nc.sync.dma_start(out=w2_raw[:], in_=w2.rearrange("(p j) d -> p j d", j=LANES))
+        load_w1(0)
         nc.sync.dma_start(offsets[:], offs)
         nc.sync.dma_start(out=sn_sb[:], in_=sn)
         cs_cols = sb.tile([P, LANES], F32, name="cs_cols", tag="late", align_bytes=64)
         with nc.allow_non_contiguous_dma(reason="one factor a partition"):
             nc.sync.dma_start(out=cs_cols[:], in_=cs[0, :].rearrange("(c p) -> p c", p=P))
-        w1_rows = w1.rearrange("(q t e) f -> e q t f", t=LANES, e=RUN)
-        for e in range(RUN):
-            nc.sync.dma_start(out=w1_raw[e:P:RUN, :, :], in_=w1_rows[e])
+        load_w1(1)
 
         dy_codes = sb.tile([P, SIZE], U32, name="dy_codes", tag="dy_codes", align_bytes=64)
         dy_scales = sb.tile([P, SIZE], U8, name="dy_scales", align_bytes=64)
@@ -135,12 +140,20 @@ def tile_attend_gbutter_pl_kernel(tc, w2, dyT, w1, cs, sn, offs, out_0, out_1, o
                 nc.tensor.transpose(own_ps[c][:, t * P : (t + 1) * P], ownT[:, t * P : (t + 1) * P], identity[:])
 
         w1_bf = [
-            sb.tile([P, 2, P, LANES], BF16, name="w1_bf%d" % h, tag=("ownT1", "late")[h], align_bytes=64) for h in range(2)
+            sb.tile([P, LANES, P // 2, LANES], BF16, name="w1_bf%d" % h, tag=("w1_early", "late")[h], align_bytes=64)
+            for h in range(2)
         ]
+        w1_codes = [sb.tile([P, P], U32, name="w1_codes0", align_bytes=64)]
         w1_scales = sb.tile([P, SIZE], U8, name="w1_scales", align_bytes=64)
-        w1_pairs = w1_raw[:].rearrange("p j (m h t) -> p h m j t", h=2, t=2)
-        for h in range(2):
-            nc.scalar.copy(out=w1_bf[h][:].rearrange("p t m j -> p m j t"), in_=w1_pairs[:, h])
+        for h, copy in enumerate((nc.vector.tensor_copy, nc.scalar.copy)):
+            copy(out=w1_bf[h][:].rearrange("p t m j -> p m j t"), in_=w1_raw[h][:].rearrange("p j (m t) -> p m j t", t=LANES))
+
+        def quantize_w1(t, h):
+            words = slice(h * P // 2, (h + 1) * P // 2)
+            cols = slice(t * P + h * P // 2, t * P + (h + 1) * P // 2)
+            quantize(w1_codes[t][:, words], w1_scales[:, cols], w1_bf[h][:, t, :, :].rearrange("p m j -> p (m j)"), E4M3)
+
+        quantize_w1(0, 0)
 
         v_codes = sb.tile([P, SIZE], U32, name="v_codes", align_bytes=64)
         v_scales = sb.tile([P, SIZE], U8, name="v_scales", align_bytes=64)
@@ -166,28 +179,26 @@ def tile_attend_gbutter_pl_kernel(tc, w2, dyT, w1, cs, sn, offs, out_0, out_1, o
             product(warm, w2_codes[:, t * P : (t + 1) * P], w2_scales[:, t * P : (t + 1) * P], dy_codes, dy_scales)
         for c in range(3):
             quantize_v(c)
-        w1_first = sb.tile([P, P], U32, name="w1_first", tag="v_bf1", align_bytes=64)
-        quantize(w1_first[:], w1_scales[:, 0:P], w1_bf[0][:, 0, :, :].rearrange("p m j -> p (m j)"), E4M3)
+        quantize_w1(0, 1)
         quantize_v(3)
-        w1_codes = [w1_first]
         for t in range(1, LANES):
             w1_codes.append(sb.tile([P, P], U32, name="w1_codes%d" % t, tag=("v_bf2", "partner", "v_bf3")[t - 1], align_bytes=64))
-            quantize(w1_codes[t][:], w1_scales[:, t * P : (t + 1) * P], w1_bf[t // 2][:, t % 2, :, :].rearrange("p m j -> p (m j)"), E4M3)
+            quantize_w1(t, 0)
+            quantize_w1(t, 1)
 
         res = sb.tile([P, LANES, SIZE], F32, name="res")
         out_rows = out_0.rearrange("(p t) x -> p t x", t=LANES)
         for t in range(LANES):
             acc = bank(4 + t, "acc%d" % t)
             product(acc, w1_codes[t][:], w1_scales[:, t * P : (t + 1) * P], v_codes, v_scales)
-            if t == LANES - 1:
-                nc.scalar.copy(out=res[:, t, 0:HALF], in_=acc[:, 0:HALF])
-                nc.scalar.copy(out=res[:, t, HALF:], in_=acc[:, HALF:])
-            elif t == 1:
-                nc.scalar.copy(out=res[:, t, :], in_=acc[:])
-            else:
-                nc.vector.tensor_copy(out=res[:, t, :], in_=acc[:])
-            if t >= 1:
-                first = 0 if t == 1 else t
+            copy = nc.vector.tensor_copy if t % 2 == 0 else nc.scalar.copy
+            pieces = ((0, HALF), (HALF, SIZE)) if t in (0, LANES - 1) else ((0, SIZE),)
+            for x0, x1 in pieces:
+                copy(out=res[:, t, x0:x1], in_=acc[:, x0:x1])
+                if t == 0:
+                    nc.sync.dma_start(out=out_rows[:, t, x0:x1], in_=res[:, t, x0:x1])
+            if t % 2 == 1:
+                first = t if t == 1 else t - 1
                 nc.sync.dma_start(out=out_rows[:, first : t + 1, :], in_=res[:, first : t + 1, :])
 
         res_codes = sb.tile([P, SIZE], U32, name="res_codes", align_bytes=64)

@@ -20,9 +20,8 @@ LANES = 4
 SIZE = 512
 SPARE = 16
 HALF = SIZE // 2
-RUN = 4
 DY_SPLIT = 320
-W2_SPLIT = 20
+W2_SPLIT = 84
 RES_SPLIT = 128
 
 FLOPS = 2 * 2 * SIZE * SIZE * SIZE
@@ -60,11 +59,10 @@ def tile_attend_gbutter_pl_kernel(tc, w2, dyT, w1, cs, sn, offs, out_0, out_1, o
         w2_raw = sb.tile([P, LANES, SIZE], F32, name="w2_raw")
         dy_raw = sb.tile([P, LANES, SIZE], F32, name="dy_raw")
         w1_raw = [sb.tile([P, LANES, HALF], F32, name="w1_raw%d" % h) for h in range(2)]
-        w1_rows = w1.rearrange("(q t e) f -> e q t f", t=LANES, e=RUN)
+        w1_rows = w1.rearrange("(p j) f -> p j f", j=LANES)
 
         def load_w1(h):
-            for e in range(RUN):
-                nc.sync.dma_start(out=w1_raw[h][e:P:RUN, :, :], in_=w1_rows[e][:, :, h * HALF : (h + 1) * HALF])
+            nc.sync.dma_start(out=w1_raw[h][:], in_=w1_rows[:, :, h * HALF : (h + 1) * HALF])
 
         sn_sb = sb.tile([P, SIZE], F32, name="sn_sb")
         nc.sync.dma_start(out=dy_raw[:], in_=dyT.rearrange("(p j) x -> p j x", j=LANES))
@@ -89,18 +87,15 @@ def tile_attend_gbutter_pl_kernel(tc, w2, dyT, w1, cs, sn, offs, out_0, out_1, o
 
         w2_codes = sb.tile([P, SIZE], U32, name="w2_codes", align_bytes=64)
         w2_scales = sb.tile([P, SIZE], U8, name="w2_scales", align_bytes=64)
-        w2_runs = w2_raw[:].rearrange("p j (q t e) -> p t q j e", t=LANES, e=RUN)
+        w2_pairs = w2_raw[:].rearrange("p j (m h t) -> p h m j t", h=2, t=2)
+        w2_bf = [sb.tile([P, 2, P, LANES], BF16, name="w2_bf%d" % h, align_bytes=64) for h in range(2)]
+        dealt = [w2_bf[h][:].rearrange("p t m j -> p m j t") for h in range(2)]
+        nc.vector.tensor_copy(out=dealt[0][:, 0:W2_SPLIT], in_=w2_pairs[:, 0, 0:W2_SPLIT])
+        nc.scalar.copy(out=dealt[0][:, W2_SPLIT:], in_=w2_pairs[:, 0, W2_SPLIT:])
+        nc.scalar.copy(out=dealt[1], in_=w2_pairs[:, 1])
         for t in range(LANES):
-            w2_bf = sb.tile([P, P, LANES], BF16, name="w2_bf%d" % t, tag="w2_bf%d" % (0, 1, 0, 3)[t], align_bytes=64)
-            cast = w2_bf[:].rearrange("p (q e) j -> p q j e", e=RUN)
-            if t == 0:
-                nc.vector.tensor_copy(out=cast[:, 0:W2_SPLIT], in_=w2_runs[:, t, 0:W2_SPLIT])
-                nc.scalar.copy(out=cast[:, W2_SPLIT:], in_=w2_runs[:, t, W2_SPLIT:])
-            else:
-                copy = nc.vector.tensor_copy if t == 2 else nc.scalar.copy
-                copy(out=cast, in_=w2_runs[:, t])
             cols = slice(t * P, (t + 1) * P)
-            quantize(w2_codes[:, cols], w2_scales[:, cols], w2_bf[:].rearrange("p m j -> p (m j)"), E4M3)
+            quantize(w2_codes[:, cols], w2_scales[:, cols], w2_bf[t // 2][:, t % 2].rearrange("p m j -> p (m j)"), E4M3)
 
         def product(acc, lhs_codes, lhs_scales, rhs_codes, rhs_scales):
             nc.tensor.matmul_mx(

@@ -18,11 +18,18 @@ SUBTRACT = mybir.AluOpType.subtract
 P = 128
 LANES = 4
 SIZE = 512
-SPARE = 16
 HALF = SIZE // 2
+CHUNKS = SIZE // P
+RUN = 4
+BAND = 16
+SPARE = 16
+
 DY_SPLIT = 320
-W2_SPLIT = 84
+W2_SPLIT = 20
 RES_SPLIT = 128
+POOL_COLS = 96
+POOL_CHUNK = CHUNKS - 1
+WARM_UPS = 2
 
 FLOPS = 2 * 2 * SIZE * SIZE * SIZE
 
@@ -30,7 +37,7 @@ FLOPS = 2 * 2 * SIZE * SIZE * SIZE
 def tile_attend_gbutter_pl_kernel(tc, w2, dyT, w1, cs, sn, offs, out_0, out_1, out_2):
     nc = tc.nc
 
-    def interleave(copy, dst, src, run=2):
+    def interleave(copy, dst, src, run):
         copy(
             out=dst.rearrange("p (c i) t -> p c t i", i=run),
             in_=src.rearrange("p t (c i) -> p c t i", i=run),
@@ -42,6 +49,20 @@ def tile_attend_gbutter_pl_kernel(tc, w2, dyT, w1, cs, sn, offs, out_0, out_1, o
     def quantize(codes, scales, words, fmt):
         nc.vector.quantize_mx(out=codes.bitcast(fmt), scales=scales, in_=words)
 
+    def product(acc, lhs_codes, lhs_scales, rhs_codes, rhs_scales):
+        nc.tensor.matmul_mx(
+            out=acc[:],
+            lhsT=lhs_codes.bitcast(E4M3),
+            lhsT_scale=lhs_scales,
+            rhs=rhs_codes[:].bitcast(E5M2),
+            rhs_scale=rhs_scales[:],
+            start=True,
+            stop=True,
+        )
+
+    def block(i):
+        return slice(i * P, (i + 1) * P)
+
     with ExitStack() as ctx:
         sb = ctx.enter_context(tc.tile_pool(name="sb", bufs=1))
         ps = ctx.enter_context(tc.psum_pool(name="ps", bufs=1))
@@ -49,7 +70,7 @@ def tile_attend_gbutter_pl_kernel(tc, w2, dyT, w1, cs, sn, offs, out_0, out_1, o
         def bank(index, name):
             return ps.tile([P, SIZE], F32, name=name, tag="bank%d" % index)
 
-        offsets = sb.tile([P, SIZE // 16], U16, name="offsets")
+        offsets = sb.tile([P, SIZE // BAND], U16, name="offsets")
         identity = sb.tile([P, P], F32, name="identity")
         make_identity(nc, identity[:])
         u_sb = [sb.tile([P, SIZE + SPARE], F32, name="u%d" % t) for t in range(LANES)]
@@ -58,24 +79,20 @@ def tile_attend_gbutter_pl_kernel(tc, w2, dyT, w1, cs, sn, offs, out_0, out_1, o
 
         w2_raw = sb.tile([P, LANES, SIZE], F32, name="w2_raw")
         dy_raw = sb.tile([P, LANES, SIZE], F32, name="dy_raw")
-        w1_raw = [sb.tile([P, LANES, HALF], F32, name="w1_raw%d" % h) for h in range(2)]
-        w1_rows = w1.rearrange("(p j) f -> p j f", j=LANES)
-
-        def load_w1(h):
-            nc.sync.dma_start(out=w1_raw[h][:], in_=w1_rows[:, :, h * HALF : (h + 1) * HALF])
-
+        w1_raw = sb.tile([P, LANES, SIZE], F32, name="w1_raw")
         sn_sb = sb.tile([P, SIZE], F32, name="sn_sb")
         nc.sync.dma_start(out=dy_raw[:], in_=dyT.rearrange("(p j) x -> p j x", j=LANES))
         nc.sync.dma_start(out=w2_raw[:], in_=w2.rearrange("(p j) d -> p j d", j=LANES))
-        load_w1(0)
         nc.sync.dma_start(offsets[:], offs)
         nc.sync.dma_start(out=sn_sb[:], in_=sn)
-        cs_cols = sb.tile([P, LANES], F32, name="cs_cols", tag="late", align_bytes=64)
+        cs_cols = sb.tile([P, CHUNKS], F32, name="cs_cols", tag="late", align_bytes=64)
         with nc.allow_non_contiguous_dma(reason="one factor a partition"):
             nc.sync.dma_start(out=cs_cols[:], in_=cs[0, :].rearrange("(c p) -> p c", p=P))
-        load_w1(1)
+        w1_rows = w1.rearrange("(q t e) f -> e q t f", t=LANES, e=RUN)
+        for e in range(RUN):
+            nc.sync.dma_start(out=w1_raw[e:P:RUN, :, :], in_=w1_rows[e])
 
-        dy_codes = sb.tile([P, SIZE], U32, name="dy_codes", tag="dy_codes", align_bytes=64)
+        dy_codes = sb.tile([P, SIZE], U32, name="dy_codes", align_bytes=64)
         dy_scales = sb.tile([P, SIZE], U8, name="dy_scales", align_bytes=64)
         dy_bf = sb.tile([P, SIZE, LANES], BF16, name="dy_bf", align_bytes=64)
         interleave(nc.vector.tensor_copy, dy_bf[:, 0:HALF, :], dy_raw[:, :, 0:HALF], 4)
@@ -87,129 +104,128 @@ def tile_attend_gbutter_pl_kernel(tc, w2, dyT, w1, cs, sn, offs, out_0, out_1, o
 
         w2_codes = sb.tile([P, SIZE], U32, name="w2_codes", align_bytes=64)
         w2_scales = sb.tile([P, SIZE], U8, name="w2_scales", align_bytes=64)
-        w2_pairs = w2_raw[:].rearrange("p j (m h t) -> p h m j t", h=2, t=2)
-        w2_bf = [sb.tile([P, 2, P, LANES], BF16, name="w2_bf%d" % h, align_bytes=64) for h in range(2)]
-        dealt = [w2_bf[h][:].rearrange("p t m j -> p m j t") for h in range(2)]
-        nc.vector.tensor_copy(out=dealt[0][:, 0:W2_SPLIT], in_=w2_pairs[:, 0, 0:W2_SPLIT])
-        nc.scalar.copy(out=dealt[0][:, W2_SPLIT:], in_=w2_pairs[:, 0, W2_SPLIT:])
-        nc.scalar.copy(out=dealt[1], in_=w2_pairs[:, 1])
+        w2_runs = w2_raw[:].rearrange("p j (q t e) -> p t q j e", t=LANES, e=RUN)
         for t in range(LANES):
-            cols = slice(t * P, (t + 1) * P)
-            quantize(w2_codes[:, cols], w2_scales[:, cols], w2_bf[t // 2][:, t % 2].rearrange("p m j -> p (m j)"), E4M3)
-
-        def product(acc, lhs_codes, lhs_scales, rhs_codes, rhs_scales):
-            nc.tensor.matmul_mx(
-                out=acc[:],
-                lhsT=lhs_codes.bitcast(E4M3),
-                lhsT_scale=lhs_scales,
-                rhs=rhs_codes[:].bitcast(E5M2),
-                rhs_scale=rhs_scales[:],
-                start=True,
-                stop=True,
-            )
+            on_vector = t % 2 == 0
+            w2_bf = sb.tile([P, P, LANES], BF16, name="w2_bf%d" % t, tag="w2_bf%d" % (0 if on_vector else t), align_bytes=64)
+            rounded = w2_bf[:].rearrange("p (q e) j -> p q j e", e=RUN)
+            if t == 0:
+                nc.vector.tensor_copy(out=rounded[:, 0:W2_SPLIT], in_=w2_runs[:, t, 0:W2_SPLIT])
+                nc.scalar.copy(out=rounded[:, W2_SPLIT:], in_=w2_runs[:, t, W2_SPLIT:])
+            else:
+                copy = nc.vector.tensor_copy if on_vector else nc.scalar.copy
+                copy(out=rounded, in_=w2_runs[:, t])
+            quantize(w2_codes[:, block(t)], w2_scales[:, block(t)], w2_bf[:].rearrange("p m j -> p (m j)"), E4M3)
 
         partner = sb.tile([P, LANES, SIZE], F32, name="partner", tag="partner", align_bytes=64)
-        uT_ps = [bank(4 + c, "uT_ps%d" % c) for c in range(4)]
+        uT_ps = [bank(LANES + c, "uT_ps%d" % c) for c in range(CHUNKS)]
         for t in range(LANES):
             u_ps = bank(t, "u_ps%d" % t)
-            product(u_ps, w2_codes[:, t * P : (t + 1) * P], w2_scales[:, t * P : (t + 1) * P], dy_codes, dy_scales)
+            product(u_ps, w2_codes[:, block(t)], w2_scales[:, block(t)], dy_codes, dy_scales)
             nc.scalar.copy(out=u_sb[t][:, 0:SIZE], in_=u_ps[:])
+
         for t in range(LANES):
             pieces = ((0, HALF), (HALF, SIZE)) if t == LANES - 1 else ((0, SIZE),)
             for x0, x1 in pieces:
-                looked_up = u_sb[t][:].indirect(offsets[:, x0 // 16 : x1 // 16])
+                looked_up = u_sb[t][:].indirect(offsets[:, x0 // BAND : x1 // BAND])
                 nc.vector.tensor_tensor(partner[:, t, x0:x1], looked_up, sn_sb[:, x0:x1], MULT)
 
-        own_ps = [None] * 4
-        for c in (3, 0, 1, 2):
+        own_order = (POOL_CHUNK,) + tuple(range(POOL_CHUNK))
+        own_ps = [None] * CHUNKS
+        for c in own_order:
             for t in range(LANES):
-                nc.tensor.transpose(uT_ps[c][:, t * P : (t + 1) * P], u_sb[t][:, c * P : (c + 1) * P], identity[:])
-        own_last = sb.tile([P, P, LANES], F32, name="own_last")
-        for c in (3, 0, 1, 2):
-            if c == 2:
-                nc.scalar.copy(out=own_last[:], in_=own_ps[3][:].rearrange("p (t x) -> p x t", t=LANES))
+                nc.tensor.transpose(uT_ps[c][:, block(t)], u_sb[t][:, block(c)], identity[:])
+        own_pool = sb.tile([P, POOL_COLS, LANES], F32, name="own_pool")
+        for c in own_order:
+            if c == own_order[-1]:
+                by_column = own_ps[POOL_CHUNK][:].rearrange("p (t x) -> p x t", t=LANES)
+                nc.scalar.copy(out=own_pool[:], in_=by_column[:, P - POOL_COLS :, :])
             ownT = sb.tile([P, SIZE], F32, name="ownT%d" % c, tag="ownT%d" % c, align_bytes=64)
             nc.scalar.activation(ownT[:], uT_ps[c][:], COPY, scale=cs_cols[:, c : c + 1])
             own_ps[c] = bank(c, "own_ps%d" % c)
             for t in range(LANES):
-                nc.tensor.transpose(own_ps[c][:, t * P : (t + 1) * P], ownT[:, t * P : (t + 1) * P], identity[:])
+                nc.tensor.transpose(own_ps[c][:, block(t)], ownT[:, block(t)], identity[:])
 
         w1_bf = [
-            sb.tile([P, LANES, P // 2, LANES], BF16, name="w1_bf%d" % h, tag=("w1_early", "late")[h], align_bytes=64)
-            for h in range(2)
+            sb.tile([P, 2, P, LANES], BF16, name="w1_bf%d" % h, tag=("ownT1", "late")[h], align_bytes=64) for h in range(2)
         ]
-        w1_codes = [sb.tile([P, P], U32, name="w1_codes0", align_bytes=64)]
         w1_scales = sb.tile([P, SIZE], U8, name="w1_scales", align_bytes=64)
-        for h, copy in enumerate((nc.vector.tensor_copy, nc.scalar.copy)):
-            copy(out=w1_bf[h][:].rearrange("p t m j -> p m j t"), in_=w1_raw[h][:].rearrange("p j (m t) -> p m j t", t=LANES))
-
-        def quantize_w1(t, h):
-            words = slice(h * P // 2, (h + 1) * P // 2)
-            cols = slice(t * P + h * P // 2, t * P + (h + 1) * P // 2)
-            quantize(w1_codes[t][:, words], w1_scales[:, cols], w1_bf[h][:, t, :, :].rearrange("p m j -> p (m j)"), E4M3)
-
-        quantize_w1(0, 0)
+        w1_pairs = w1_raw[:].rearrange("p j (r h t) -> p h r j t", h=2, t=2)
+        for h in range(2):
+            nc.scalar.copy(out=w1_bf[h][:].rearrange("p t r j -> p r j t"), in_=w1_pairs[:, h])
 
         v_codes = sb.tile([P, SIZE], U32, name="v_codes", align_bytes=64)
         v_scales = sb.tile([P, SIZE], U8, name="v_scales", align_bytes=64)
-        v_bf = [sb.tile([P, P, LANES], BF16, name="v_bf%d" % c, tag="v_bf%d" % c, align_bytes=64) for c in range(4)]
+        v_bf = [sb.tile([P, P, LANES], BF16, name="v_bf%d" % c, tag="v_bf%d" % c, align_bytes=64) for c in range(CHUNKS)]
 
-        def mix(c):
+        def mix(c, n):
             nc.vector.tensor_tensor(
-                v_bf[c][:].rearrange("p (c i) t -> p c t i", i=2),
-                own_ps[c][:].rearrange("p (t c i) -> p c t i", t=LANES, i=2),
-                partner[:, :, c * P : (c + 1) * P].rearrange("p t (c i) -> p c t i", i=2),
+                v_bf[c][:, 0:n, :].rearrange("p (c i) t -> p c t i", i=2),
+                own_ps[c][:].rearrange("p (t x) -> p t x", t=LANES)[:, :, 0:n].rearrange("p t (c i) -> p c t i", i=2),
+                partner[:, :, c * P : c * P + n].rearrange("p t (c i) -> p c t i", i=2),
                 SUBTRACT,
             )
 
         def quantize_v(c):
-            cols = slice(c * P, (c + 1) * P)
-            quantize(v_codes[:, cols], v_scales[:, cols], v_bf[c][:].rearrange("p x t -> p (x t)"), E5M2)
+            quantize(v_codes[:, block(c)], v_scales[:, block(c)], v_bf[c][:].rearrange("p x t -> p (x t)"), E5M2)
 
-        nc.gpsimd.tensor_tensor(v_bf[3][:], own_last[:], partner[:, :, 3 * P :].rearrange("p t x -> p x t"), SUBTRACT)
-        for c in range(3):
-            mix(c)
-        warm = bank(1, "warm")
-        for t in range(2):
-            product(warm, w2_codes[:, t * P : (t + 1) * P], w2_scales[:, t * P : (t + 1) * P], dy_codes, dy_scales)
-        for c in range(3):
+        def quantize_w1(t, tag):
+            codes = sb.tile([P, P], U32, name="w1_codes%d" % t, tag=tag, align_bytes=64)
+            quantize(codes[:], w1_scales[:, block(t)], w1_bf[t // 2][:, t % 2, :, :].rearrange("p r j -> p (r j)"), E4M3)
+            return codes
+
+        nc.gpsimd.tensor_tensor(
+            v_bf[POOL_CHUNK][:, P - POOL_COLS :, :],
+            own_pool[:],
+            partner[:, :, SIZE - POOL_COLS :].rearrange("p t x -> p x t"),
+            SUBTRACT,
+        )
+        mix(0, P)
+        mix(POOL_CHUNK, P - POOL_COLS)
+        for c in range(1, POOL_CHUNK):
+            mix(c, P)
+
+        warm = bank(POOL_CHUNK, "warm")
+        for t in range(WARM_UPS):
+            product(warm, w2_codes[:, block(t)], w2_scales[:, block(t)], dy_codes, dy_scales)
+
+        for c in range(POOL_CHUNK):
             quantize_v(c)
-        quantize_w1(0, 1)
-        quantize_v(3)
-        for t in range(1, LANES):
-            w1_codes.append(sb.tile([P, P], U32, name="w1_codes%d" % t, tag=("v_bf2", "partner", "v_bf3")[t - 1], align_bytes=64))
-            quantize_w1(t, 0)
-            quantize_w1(t, 1)
+        w1_codes = [quantize_w1(0, "v_bf1")]
+        quantize_v(POOL_CHUNK)
+        for t, tag in ((1, "v_bf2"), (2, "partner"), (3, "v_bf3")):
+            w1_codes.append(quantize_w1(t, tag))
 
-        res = sb.tile([P, LANES, SIZE], F32, name="res")
+        res = sb.tile([P, LANES, SIZE], F32, name="res", tag="late", align_bytes=64)
         out_rows = out_0.rearrange("(p t) x -> p t x", t=LANES)
         for t in range(LANES):
-            acc = bank(4 + t, "acc%d" % t)
-            product(acc, w1_codes[t][:], w1_scales[:, t * P : (t + 1) * P], v_codes, v_scales)
+            acc = bank(LANES + t, "acc%d" % t)
+            product(acc, w1_codes[t][:], w1_scales[:, block(t)], v_codes, v_scales)
             copy = nc.vector.tensor_copy if t % 2 == 0 else nc.scalar.copy
             pieces = ((0, HALF), (HALF, SIZE)) if t in (0, LANES - 1) else ((0, SIZE),)
             for x0, x1 in pieces:
                 copy(out=res[:, t, x0:x1], in_=acc[:, x0:x1])
                 if t == 0:
                     nc.sync.dma_start(out=out_rows[:, t, x0:x1], in_=res[:, t, x0:x1])
-            if t % 2 == 1:
-                first = t if t == 1 else t - 1
-                nc.sync.dma_start(out=out_rows[:, first : t + 1, :], in_=res[:, first : t + 1, :])
+            if t == 1:
+                nc.sync.dma_start(out=out_rows[:, 1:2, :], in_=res[:, 1:2, :])
+            if t == LANES - 1:
+                nc.sync.dma_start(out=out_rows[:, 2:, :], in_=res[:, 2:, :])
 
         res_codes = sb.tile([P, SIZE], U32, name="res_codes", align_bytes=64)
         res_scales = sb.tile([P, SIZE], U8, name="res_scales", align_bytes=64)
         res_bf = [sb.tile([P, HALF, LANES], BF16, name="res_bf%d" % h, align_bytes=64) for h in range(2)]
         out_words = out_1[0].rearrange("p x l -> p (x l)").bitcast(I32)
-        interleave(nc.vector.tensor_copy, res_bf[0][:], res[:, :, 0:HALF])
-        interleave(nc.vector.tensor_copy, res_bf[1][:, 0:RES_SPLIT, :], res[:, :, HALF : HALF + RES_SPLIT])
-        interleave(nc.scalar.copy, res_bf[1][:, RES_SPLIT:, :], res[:, :, HALF + RES_SPLIT : SIZE])
+        interleave(nc.vector.tensor_copy, res_bf[0][:], res[:, :, 0:HALF], 2)
+        interleave(nc.vector.tensor_copy, res_bf[1][:, 0:RES_SPLIT, :], res[:, :, HALF : HALF + RES_SPLIT], 2)
+        interleave(nc.scalar.copy, res_bf[1][:, RES_SPLIT:, :], res[:, :, HALF + RES_SPLIT : SIZE], 2)
         for h in range(2):
             cols = slice(h * HALF, (h + 1) * HALF)
             quantize(res_codes[:, cols], res_scales[:, cols], res_bf[h][:].rearrange("p x t -> p (x t)"), E4M3)
             nc.sync.dma_start(out=out_words[:, cols], in_=res_codes[:, cols].bitcast(I32))
-        for q in range(4):
-            queue = nc.sync if q % 2 == 0 else nc.scalar
+        for quad in range(4):
+            queue = nc.sync if quad % 2 == 0 else nc.scalar
             queue.dma_start(
-                out=out_2[0, 4 * q : 4 * q + 4, :].bitcast(I32),
-                in_=res_scales[32 * q : 32 * q + 4, :].bitcast(I32),
+                out=out_2[0, 4 * quad : 4 * quad + 4, :].bitcast(I32),
+                in_=res_scales[32 * quad : 32 * quad + 4, :].bitcast(I32),
             )

@@ -25,10 +25,10 @@ BAND = 16
 SPARE = 16
 
 DY_SPLIT = 320
-W2_SPLIT = 20
+W2_SPLIT = 6
 RES_SPLIT = 128
 POOL_COLS = 96
-POOL_CHUNK = CHUNKS - 1
+POOL_CHUNK = 1
 WARM_UPS = 2
 
 FLOPS = 2 * 2 * SIZE * SIZE * SIZE
@@ -77,13 +77,15 @@ def tile_attend_gbutter_pl_kernel(tc, w2, dyT, w1, cs, sn, offs, out_0, out_1, o
         for t in range(LANES):
             nc.gpsimd.memset(u_sb[t][:, SIZE:], 0.0)
 
-        w2_raw = sb.tile([P, LANES, SIZE], F32, name="w2_raw")
+        w2_raw = [sb.tile([P, LANES, HALF], F32, name="w2_raw%d" % h) for h in range(2)]
         dy_raw = sb.tile([P, LANES, SIZE], F32, name="dy_raw")
         w1_raw = sb.tile([P, LANES, SIZE], F32, name="w1_raw")
         sn_sb = sb.tile([P, SIZE], F32, name="sn_sb")
         nc.sync.dma_start(out=dy_raw[:], in_=dyT.rearrange("(p j) x -> p j x", j=LANES))
-        nc.sync.dma_start(out=w2_raw[:], in_=w2.rearrange("(p j) d -> p j d", j=LANES))
+        w2_rows = w2.rearrange("(p j) d -> p j d", j=LANES)
+        nc.sync.dma_start(out=w2_raw[0][:], in_=w2_rows[:, :, 0:HALF])
         nc.sync.dma_start(offsets[:], offs)
+        nc.sync.dma_start(out=w2_raw[1][:], in_=w2_rows[:, :, HALF:])
         nc.sync.dma_start(out=sn_sb[:], in_=sn)
         cs_cols = sb.tile([P, CHUNKS], F32, name="cs_cols", tag="late", align_bytes=64)
         with nc.allow_non_contiguous_dma(reason="one factor a partition"):
@@ -104,18 +106,25 @@ def tile_attend_gbutter_pl_kernel(tc, w2, dyT, w1, cs, sn, offs, out_0, out_1, o
 
         w2_codes = sb.tile([P, SIZE], U32, name="w2_codes", align_bytes=64)
         w2_scales = sb.tile([P, SIZE], U8, name="w2_scales", align_bytes=64)
-        w2_runs = w2_raw[:].rearrange("p j (q t e) -> p t q j e", t=LANES, e=RUN)
-        for t in range(LANES):
-            on_vector = t % 2 == 0
-            w2_bf = sb.tile([P, P, LANES], BF16, name="w2_bf%d" % t, tag="w2_bf%d" % (0 if on_vector else t), align_bytes=64)
-            rounded = w2_bf[:].rearrange("p (q e) j -> p q j e", e=RUN)
-            if t == 0:
-                nc.vector.tensor_copy(out=rounded[:, 0:W2_SPLIT], in_=w2_runs[:, t, 0:W2_SPLIT])
-                nc.scalar.copy(out=rounded[:, W2_SPLIT:], in_=w2_runs[:, t, W2_SPLIT:])
+        w2_runs = [w2_raw[h][:].rearrange("p j (q t e) -> p t q j e", t=LANES, e=RUN) for h in range(2)]
+        w2_first = [sb.tile([P, P, LANES], BF16, name="w2_first%d" % h, align_bytes=64) for h in range(2)]
+        w2_last = sb.tile([P, 2, P, LANES], BF16, name="w2_last", align_bytes=64)
+        last_runs = w2_last[:].rearrange("p t (h q e) j -> p h t q j e", h=2, e=RUN)
+
+        def quantize_w2(g, words):
+            quantize(w2_codes[:, block(g)], w2_scales[:, block(g)], words.rearrange("p m j -> p (m j)"), E4M3)
+
+        for h in range(2):
+            rounded = w2_first[h][:].rearrange("p (t q e) j -> p t q j e", t=2, e=RUN)
+            if h == 0:
+                nc.vector.tensor_copy(out=rounded[:, :, 0:W2_SPLIT], in_=w2_runs[h][:, 0:2, 0:W2_SPLIT])
+                nc.scalar.copy(out=rounded[:, :, W2_SPLIT:], in_=w2_runs[h][:, 0:2, W2_SPLIT:])
             else:
-                copy = nc.vector.tensor_copy if on_vector else nc.scalar.copy
-                copy(out=rounded, in_=w2_runs[:, t])
-            quantize(w2_codes[:, block(t)], w2_scales[:, block(t)], w2_bf[:].rearrange("p m j -> p (m j)"), E4M3)
+                nc.vector.tensor_copy(out=rounded, in_=w2_runs[h][:, 0:2])
+            quantize_w2(h, w2_first[h][:])
+            nc.scalar.copy(out=last_runs[:, h], in_=w2_runs[h][:, 2:])
+        for t in range(2):
+            quantize_w2(2 + t, w2_last[:, t])
 
         partner = sb.tile([P, LANES, SIZE], F32, name="partner", tag="partner", align_bytes=64)
         uT_ps = [bank(LANES + c, "uT_ps%d" % c) for c in range(CHUNKS)]
@@ -124,17 +133,28 @@ def tile_attend_gbutter_pl_kernel(tc, w2, dyT, w1, cs, sn, offs, out_0, out_1, o
             product(u_ps, w2_codes[:, block(t)], w2_scales[:, block(t)], dy_codes, dy_scales)
             nc.scalar.copy(out=u_sb[t][:, 0:SIZE], in_=u_ps[:])
 
+        moved = [sb.tile([P, SIZE], F32, name="moved%d" % h) for h in range(2)]
+        halves = (slice(0, P // 2), slice(P // 2, P))
         for t in range(LANES):
-            pieces = ((0, HALF), (HALF, SIZE)) if t == LANES - 1 else ((0, SIZE),)
+            pieces = {1: ((0, HALF), (HALF, SIZE)), LANES - 1: ((0, P), (P, SIZE))}.get(t, ((0, SIZE),))
             for x0, x1 in pieces:
                 looked_up = u_sb[t][:].indirect(offsets[:, x0 // BAND : x1 // BAND])
-                nc.vector.tensor_tensor(partner[:, t, x0:x1], looked_up, sn_sb[:, x0:x1], MULT)
+                target = moved[t][:, x0:x1] if t < 2 else partner[:, t, x0:x1]
+                nc.vector.tensor_tensor(target, looked_up, sn_sb[:, x0:x1], MULT)
+                if t < 2:
+                    for lane in range(2):
+                        nc.sync.dma_start(out=partner[halves[t], lane, x0:x1], in_=moved[t][halves[lane], x0:x1])
 
-        own_order = (POOL_CHUNK,) + tuple(range(POOL_CHUNK))
+        others = tuple(c for c in range(CHUNKS) if c != POOL_CHUNK)
+        own_order = (POOL_CHUNK,) + others
         own_ps = [None] * CHUNKS
         for c in own_order:
             for t in range(LANES):
-                nc.tensor.transpose(uT_ps[c][:, block(t)], u_sb[t][:, block(c)], identity[:])
+                if t < 2:
+                    turned = uT_ps[c][:].rearrange("p (t h i) -> p h t i", t=LANES, h=2)[:, t, 0:2, :]
+                else:
+                    turned = uT_ps[c][:, block(t)]
+                nc.tensor.transpose(turned, u_sb[t][:, block(c)], identity[:])
         own_pool = sb.tile([P, POOL_COLS, LANES], F32, name="own_pool")
         for c in own_order:
             if c == own_order[-1]:
@@ -147,7 +167,7 @@ def tile_attend_gbutter_pl_kernel(tc, w2, dyT, w1, cs, sn, offs, out_0, out_1, o
                 nc.tensor.transpose(own_ps[c][:, block(t)], ownT[:, block(t)], identity[:])
 
         w1_bf = [
-            sb.tile([P, 2, P, LANES], BF16, name="w1_bf%d" % h, tag=("ownT1", "late")[h], align_bytes=64) for h in range(2)
+            sb.tile([P, 2, P, LANES], BF16, name="w1_bf%d" % h, tag=("ownT%d" % others[1], "late")[h], align_bytes=64) for h in range(2)
         ]
         w1_scales = sb.tile([P, SIZE], U8, name="w1_scales", align_bytes=64)
         w1_pairs = w1_raw[:].rearrange("p j (r h t) -> p h r j t", h=2, t=2)
@@ -177,23 +197,23 @@ def tile_attend_gbutter_pl_kernel(tc, w2, dyT, w1, cs, sn, offs, out_0, out_1, o
         nc.gpsimd.tensor_tensor(
             v_bf[POOL_CHUNK][:, P - POOL_COLS :, :],
             own_pool[:],
-            partner[:, :, SIZE - POOL_COLS :].rearrange("p t x -> p x t"),
+            partner[:, :, (POOL_CHUNK + 1) * P - POOL_COLS : (POOL_CHUNK + 1) * P].rearrange("p t x -> p x t"),
             SUBTRACT,
         )
         mix(0, P)
         mix(POOL_CHUNK, P - POOL_COLS)
-        for c in range(1, POOL_CHUNK):
+        for c in others[1:]:
             mix(c, P)
 
         warm = bank(POOL_CHUNK, "warm")
         for t in range(WARM_UPS):
             product(warm, w2_codes[:, block(t)], w2_scales[:, block(t)], dy_codes, dy_scales)
 
-        for c in range(POOL_CHUNK):
+        for c in others:
             quantize_v(c)
-        w1_codes = [quantize_w1(0, "v_bf1")]
+        w1_codes = [quantize_w1(0, "v_bf%d" % others[1])]
         quantize_v(POOL_CHUNK)
-        for t, tag in ((1, "v_bf2"), (2, "partner"), (3, "v_bf3")):
+        for t, tag in ((1, "v_bf%d" % others[2]), (2, "partner"), (3, "v_bf%d" % POOL_CHUNK)):
             w1_codes.append(quantize_w1(t, tag))
 
         res = sb.tile([P, LANES, SIZE], F32, name="res", tag="late", align_bytes=64)

@@ -20,12 +20,13 @@ LANES = 4
 SIZE = 512
 HALF = SIZE // 2
 CHUNKS = SIZE // P
-RUN = 4
 BAND = 16
 SPARE = 16
 
 DY_SPLIT = 320
-W2_SPLIT = 6
+W1_EARLY = 128
+W1_PIECE = 16
+W2_SPLIT = 24
 RES_SPLIT = 128
 POOL_COLS = 96
 POOL_CHUNK = 1
@@ -79,20 +80,21 @@ def tile_attend_gbutter_pl_kernel(tc, w2, dyT, w1, cs, sn, offs, out_0, out_1, o
 
         w2_raw = [sb.tile([P, LANES, HALF], F32, name="w2_raw%d" % h) for h in range(2)]
         dy_raw = sb.tile([P, LANES, SIZE], F32, name="dy_raw")
-        w1_raw = sb.tile([P, LANES, SIZE], F32, name="w1_raw")
+        w1_early = sb.tile([P, LANES, W1_EARLY], F32, name="w1_early")
+        w1_raw = sb.tile([P, LANES, SIZE - W1_EARLY], F32, name="w1_raw")
+        w1_rows = w1.rearrange("(p j) f -> p j f", j=LANES)
         sn_sb = sb.tile([P, SIZE], F32, name="sn_sb")
         nc.sync.dma_start(out=dy_raw[:], in_=dyT.rearrange("(p j) x -> p j x", j=LANES))
         w2_rows = w2.rearrange("(p j) d -> p j d", j=LANES)
         nc.sync.dma_start(out=w2_raw[0][:], in_=w2_rows[:, :, 0:HALF])
         nc.sync.dma_start(offsets[:], offs)
         nc.sync.dma_start(out=w2_raw[1][:], in_=w2_rows[:, :, HALF:])
+        nc.sync.dma_start(out=w1_early[:], in_=w1_rows[:, :, SIZE - W1_EARLY :])
         nc.sync.dma_start(out=sn_sb[:], in_=sn)
-        cs_cols = sb.tile([P, CHUNKS], F32, name="cs_cols", tag="late", align_bytes=64)
+        cs_cols = sb.tile([P, CHUNKS], F32, name="cs_cols")
         with nc.allow_non_contiguous_dma(reason="one factor a partition"):
             nc.sync.dma_start(out=cs_cols[:], in_=cs[0, :].rearrange("(c p) -> p c", p=P))
-        w1_rows = w1.rearrange("(q t e) f -> e q t f", t=LANES, e=RUN)
-        for e in range(RUN):
-            nc.sync.dma_start(out=w1_raw[e:P:RUN, :, :], in_=w1_rows[e])
+        nc.sync.dma_start(out=w1_raw[:], in_=w1_rows[:, :, 0 : SIZE - W1_EARLY])
 
         dy_codes = sb.tile([P, SIZE], U32, name="dy_codes", align_bytes=64)
         dy_scales = sb.tile([P, SIZE], U8, name="dy_scales", align_bytes=64)
@@ -106,25 +108,31 @@ def tile_attend_gbutter_pl_kernel(tc, w2, dyT, w1, cs, sn, offs, out_0, out_1, o
 
         w2_codes = sb.tile([P, SIZE], U32, name="w2_codes", align_bytes=64)
         w2_scales = sb.tile([P, SIZE], U8, name="w2_scales", align_bytes=64)
-        w2_runs = [w2_raw[h][:].rearrange("p j (q t e) -> p t q j e", t=LANES, e=RUN) for h in range(2)]
+        w2_quads = [w2_raw[h][:].rearrange("p j (i t) -> p i j t", t=LANES) for h in range(2)]
         w2_first = [sb.tile([P, P, LANES], BF16, name="w2_first%d" % h, align_bytes=64) for h in range(2)]
         w2_last = sb.tile([P, 2, P, LANES], BF16, name="w2_last", align_bytes=64)
-        last_runs = w2_last[:].rearrange("p t (h q e) j -> p h t q j e", h=2, e=RUN)
+        last_dealt = w2_last[:].rearrange("p t (h i) j -> p h i j t", h=2)
 
         def quantize_w2(g, words):
             quantize(w2_codes[:, block(g)], w2_scales[:, block(g)], words.rearrange("p m j -> p (m j)"), E4M3)
 
+        def shared(dst, src, n):
+            if n > 0:
+                nc.vector.tensor_copy(out=dst[:, 0:n], in_=src[:, 0:n])
+            if n < P // 2:
+                nc.scalar.copy(out=dst[:, n:], in_=src[:, n:])
+
         for h in range(2):
-            rounded = w2_first[h][:].rearrange("p (t q e) j -> p t q j e", t=2, e=RUN)
-            if h == 0:
-                nc.vector.tensor_copy(out=rounded[:, :, 0:W2_SPLIT], in_=w2_runs[h][:, 0:2, 0:W2_SPLIT])
-                nc.scalar.copy(out=rounded[:, :, W2_SPLIT:], in_=w2_runs[h][:, 0:2, W2_SPLIT:])
-            else:
-                nc.vector.tensor_copy(out=rounded, in_=w2_runs[h][:, 0:2])
+            first_dealt = w2_first[h][:].rearrange("p (t i) j -> p i j t", t=2)
+            shared(first_dealt, w2_quads[h][:, :, :, 0:2], (W2_SPLIT, P // 2)[h])
+            shared(last_dealt[:, h], w2_quads[h][:, :, :, 2:], (0, P // 4)[h])
             quantize_w2(h, w2_first[h][:])
-            nc.scalar.copy(out=last_runs[:, h], in_=w2_runs[h][:, 2:])
         for t in range(2):
             quantize_w2(2 + t, w2_last[:, t])
+        w1_bf = sb.tile([P, LANES, P, LANES], BF16, name="w1_bf", tag="late", align_bytes=64)
+        w1_dealt = w1_bf[:].rearrange("p t r j -> p r j t")
+        late_words = (SIZE - W1_EARLY) // LANES
+        nc.vector.tensor_copy(out=w1_dealt[:, late_words:], in_=w1_early[:].rearrange("p j (r t) -> p r j t", t=LANES))
 
         partner = sb.tile([P, LANES, SIZE], F32, name="partner", tag="partner", align_bytes=64)
         uT_ps = [bank(LANES + c, "uT_ps%d" % c) for c in range(CHUNKS)]
@@ -166,13 +174,10 @@ def tile_attend_gbutter_pl_kernel(tc, w2, dyT, w1, cs, sn, offs, out_0, out_1, o
             for t in range(LANES):
                 nc.tensor.transpose(own_ps[c][:, block(t)], ownT[:, block(t)], identity[:])
 
-        w1_bf = [
-            sb.tile([P, 2, P, LANES], BF16, name="w1_bf%d" % h, tag=("ownT%d" % others[1], "late")[h], align_bytes=64) for h in range(2)
-        ]
         w1_scales = sb.tile([P, SIZE], U8, name="w1_scales", align_bytes=64)
-        w1_pairs = w1_raw[:].rearrange("p j (r h t) -> p h r j t", h=2, t=2)
-        for h in range(2):
-            nc.scalar.copy(out=w1_bf[h][:].rearrange("p t r j -> p r j t"), in_=w1_pairs[:, h])
+        w1_quads = w1_raw[:].rearrange("p j (r t) -> p r j t", t=LANES)
+        for r0 in range(0, late_words, W1_PIECE):
+            nc.scalar.copy(out=w1_dealt[:, r0 : r0 + W1_PIECE], in_=w1_quads[:, r0 : r0 + W1_PIECE])
 
         v_codes = sb.tile([P, SIZE], U32, name="v_codes", align_bytes=64)
         v_scales = sb.tile([P, SIZE], U8, name="v_scales", align_bytes=64)
@@ -191,7 +196,7 @@ def tile_attend_gbutter_pl_kernel(tc, w2, dyT, w1, cs, sn, offs, out_0, out_1, o
 
         def quantize_w1(t, tag):
             codes = sb.tile([P, P], U32, name="w1_codes%d" % t, tag=tag, align_bytes=64)
-            quantize(codes[:], w1_scales[:, block(t)], w1_bf[t // 2][:, t % 2, :, :].rearrange("p r j -> p (r j)"), E4M3)
+            quantize(codes[:], w1_scales[:, block(t)], w1_bf[:, t, :, :].rearrange("p r j -> p (r j)"), E4M3)
             return codes
 
         nc.gpsimd.tensor_tensor(

@@ -26,6 +26,7 @@ SPARE = 16
 DY_SPLIT = 320
 W1_EARLY = 128
 W1_PIECE = 16
+PAD = 8
 W2_SPLIT = 24
 RES_SPLIT = 128
 POOL_COLS = 96
@@ -78,10 +79,10 @@ def tile_attend_gbutter_pl_kernel(tc, w2, dyT, w1, cs, sn, offs, out_0, out_1, o
         for t in range(LANES):
             nc.gpsimd.memset(u_sb[t][:, SIZE:], 0.0)
 
-        w2_raw = [sb.tile([P, LANES, HALF], F32, name="w2_raw%d" % h) for h in range(2)]
+        w2_raw = [sb.tile([P, LANES, HALF + PAD], F32, name="w2_raw%d" % h)[:, :, 0:HALF] for h in range(2)]
         dy_raw = sb.tile([P, LANES, SIZE], F32, name="dy_raw")
-        w1_early = sb.tile([P, LANES, W1_EARLY], F32, name="w1_early")
-        w1_raw = sb.tile([P, LANES, SIZE - W1_EARLY], F32, name="w1_raw")
+        w1_early = sb.tile([P, LANES, W1_EARLY + PAD], F32, name="w1_early")[:, :, 0:W1_EARLY]
+        w1_raw = sb.tile([P, LANES, SIZE - W1_EARLY + PAD], F32, name="w1_raw")[:, :, 0 : SIZE - W1_EARLY]
         w1_rows = w1.rearrange("(p j) f -> p j f", j=LANES)
         sn_sb = sb.tile([P, SIZE], F32, name="sn_sb")
         nc.sync.dma_start(out=dy_raw[:], in_=dyT.rearrange("(p j) x -> p j x", j=LANES))
@@ -129,12 +130,12 @@ def tile_attend_gbutter_pl_kernel(tc, w2, dyT, w1, cs, sn, offs, out_0, out_1, o
             quantize_w2(h, w2_first[h][:])
         for t in range(2):
             quantize_w2(2 + t, w2_last[:, t])
-        w1_bf = sb.tile([P, LANES, P, LANES], BF16, name="w1_bf", tag="late", align_bytes=64)
+        w1_bf = sb.tile([P, LANES, P + PAD, LANES], BF16, name="w1_bf", tag="late", align_bytes=64)[:, :, 0:P, :]
         w1_dealt = w1_bf[:].rearrange("p t r j -> p r j t")
         late_words = (SIZE - W1_EARLY) // LANES
         nc.vector.tensor_copy(out=w1_dealt[:, late_words:], in_=w1_early[:].rearrange("p j (r t) -> p r j t", t=LANES))
 
-        partner = sb.tile([P, LANES, SIZE], F32, name="partner", tag="partner", align_bytes=64)
+        partner = sb.tile([P, LANES, SIZE + PAD], F32, name="partner", tag="partner", align_bytes=64)[:, :, 0:SIZE]
         uT_ps = [bank(LANES + c, "uT_ps%d" % c) for c in range(CHUNKS)]
         for t in range(LANES):
             u_ps = bank(t, "u_ps%d" % t)

@@ -25,6 +25,7 @@ SPARE = 16
 
 DY_SPLIT = 320
 W1_EARLY = 128
+FIRST = HALF + 8
 W1_PIECE = 16
 PAD = 8
 W2_SPLIT = 24
@@ -100,8 +101,8 @@ def tile_attend_gbutter_pl_kernel(tc, w2, dyT, w1, cs, sn, offs, out_0, out_1, o
         dy_codes = sb.tile([P, SIZE], U32, name="dy_codes", align_bytes=64)
         dy_scales = sb.tile([P, SIZE], U8, name="dy_scales", align_bytes=64)
         dy_bf = sb.tile([P, SIZE, LANES], BF16, name="dy_bf", align_bytes=64)
-        interleave(nc.vector.tensor_copy, dy_bf[:, 0:HALF, :], dy_raw[:, :, 0:HALF], 4)
-        interleave(nc.vector.tensor_copy, dy_bf[:, HALF:DY_SPLIT, :], dy_raw[:, :, HALF:DY_SPLIT], 4)
+        interleave(nc.vector.tensor_copy, dy_bf[:, 0:FIRST, :], dy_raw[:, :, 0:FIRST], 4)
+        interleave(nc.vector.tensor_copy, dy_bf[:, FIRST:DY_SPLIT, :], dy_raw[:, :, FIRST:DY_SPLIT], 4)
         interleave(scalar_cast, dy_bf[:, DY_SPLIT:, :], dy_raw[:, :, DY_SPLIT:], 4)
         for h in range(2):
             cols = slice(h * HALF, (h + 1) * HALF)
@@ -228,7 +229,7 @@ def tile_attend_gbutter_pl_kernel(tc, w2, dyT, w1, cs, sn, offs, out_0, out_1, o
             acc = bank(LANES + t, "acc%d" % t)
             product(acc, w1_codes[t][:], w1_scales[:, block(t)], v_codes, v_scales)
             copy = nc.vector.tensor_copy if t % 2 == 0 else nc.scalar.copy
-            pieces = ((0, HALF), (HALF, SIZE)) if t in (0, LANES - 1) else ((0, SIZE),)
+            pieces = {0: ((0, HALF), (HALF, SIZE)), LANES - 1: ((0, FIRST), (FIRST, SIZE))}.get(t, ((0, SIZE),))
             for x0, x1 in pieces:
                 copy(out=res[:, t, x0:x1], in_=acc[:, x0:x1])
                 if t == 0:
@@ -240,14 +241,15 @@ def tile_attend_gbutter_pl_kernel(tc, w2, dyT, w1, cs, sn, offs, out_0, out_1, o
 
         res_codes = sb.tile([P, SIZE], U32, name="res_codes", align_bytes=64)
         res_scales = sb.tile([P, SIZE], U8, name="res_scales", align_bytes=64)
-        res_bf = [sb.tile([P, HALF, LANES], BF16, name="res_bf%d" % h, align_bytes=64) for h in range(2)]
+        res_bf = sb.tile([P, SIZE, LANES], BF16, name="res_bf", align_bytes=64)
         out_words = out_1[0].rearrange("p x l -> p (x l)").bitcast(I32)
-        interleave(nc.vector.tensor_copy, res_bf[0][:], res[:, :, 0:HALF], 2)
-        interleave(nc.vector.tensor_copy, res_bf[1][:, 0:RES_SPLIT, :], res[:, :, HALF : HALF + RES_SPLIT], 2)
-        interleave(nc.scalar.copy, res_bf[1][:, RES_SPLIT:, :], res[:, :, HALF + RES_SPLIT : SIZE], 2)
+        split = HALF + RES_SPLIT
+        interleave(nc.vector.tensor_copy, res_bf[:, 0:FIRST, :], res[:, :, 0:FIRST], 2)
+        interleave(nc.vector.tensor_copy, res_bf[:, FIRST:split, :], res[:, :, FIRST:split], 2)
+        interleave(nc.scalar.copy, res_bf[:, split:, :], res[:, :, split:SIZE], 2)
         for h in range(2):
             cols = slice(h * HALF, (h + 1) * HALF)
-            quantize(res_codes[:, cols], res_scales[:, cols], res_bf[h][:].rearrange("p x t -> p (x t)"), E4M3)
+            quantize(res_codes[:, cols], res_scales[:, cols], res_bf[:, cols, :].rearrange("p x t -> p (x t)"), E4M3)
             nc.sync.dma_start(out=out_words[:, cols], in_=res_codes[:, cols].bitcast(I32))
         for quad in range(4):
             queue = nc.sync if quad % 2 == 0 else nc.scalar

from contextlib import ExitStack

import concourse.mybir as mybir
from concourse.masks import make_identity

F32 = mybir.dt.float32
BF16 = mybir.dt.bfloat16
I32 = mybir.dt.int32
U32 = mybir.dt.uint32
U16 = mybir.dt.uint16
U8 = mybir.dt.uint8
E4M3 = mybir.dt.float8_e4m3fn_x4
E5M2 = mybir.dt.float8_e5m2_x4
COPY = mybir.ActivationFunctionType.Copy
MULT = mybir.AluOpType.mult
SUBTRACT = mybir.AluOpType.subtract

P = 128
LANES = 4
SIZE = 512
HALF = SIZE // 2
CHUNKS = SIZE // P
BAND = 16
SPARE = 16

DY_SPLIT = 320
W1_EARLY = 128
FIRST = HALF + 8
W1_PIECE = 16
PAD = 8
W2_SPLIT = 24
RES_SPLIT = 128
POOL_COLS = 96
POOL_CHUNK = 1
WARM_UPS = 2

FLOPS = 2 * 2 * SIZE * SIZE * SIZE


def tile_attend_gbutter_pl_kernel(tc, w2, dyT, w1, cs, sn, offs, out_0, out_1, out_2):
    nc = tc.nc

    def interleave(copy, dst, src, run):
        copy(
            out=dst.rearrange("p (c i) t -> p c t i", i=run),
            in_=src.rearrange("p t (c i) -> p c t i", i=run),
        )

    def scalar_cast(out, in_):
        nc.scalar.activation(out, in_, COPY)

    def quantize(codes, scales, words, fmt):
        nc.vector.quantize_mx(out=codes.bitcast(fmt), scales=scales, in_=words)

    def product(acc, lhs_codes, lhs_scales, rhs_codes, rhs_scales):
        nc.tensor.matmul_mx(
            out=acc[:],
            lhsT=lhs_codes.bitcast(E4M3),
            lhsT_scale=lhs_scales,
            rhs=rhs_codes[:].bitcast(E5M2),
            rhs_scale=rhs_scales[:],
            start=True,
            stop=True,
        )

    def block(i):
        return slice(i * P, (i + 1) * P)

    with ExitStack() as ctx:
        sb = ctx.enter_context(tc.tile_pool(name="sb", bufs=1))
        ps = ctx.enter_context(tc.psum_pool(name="ps", bufs=1))

        def bank(index, name):
            return ps.tile([P, SIZE], F32, name=name, tag="bank%d" % index)

        offsets = sb.tile([P, SIZE // BAND], U16, name="offsets")
        identity = sb.tile([P, P], F32, name="identity")
        make_identity(nc, identity[:])
        u_sb = [sb.tile([P, SIZE + SPARE], F32, name="u%d" % t) for t in range(LANES)]
        for t in range(LANES):
            nc.gpsimd.memset(u_sb[t][:, SIZE:], 0.0)

        w2_raw = [sb.tile([P, LANES, HALF + PAD], F32, name="w2_raw%d" % h)[:, :, 0:HALF] for h in range(2)]
        dy_raw = sb.tile([P, LANES, SIZE], F32, name="dy_raw")
        w1_early = sb.tile([P, LANES, W1_EARLY + PAD], F32, name="w1_early")[:, :, 0:W1_EARLY]
        w1_raw = sb.tile([P, LANES, SIZE - W1_EARLY + PAD], F32, name="w1_raw")[:, :, 0 : SIZE - W1_EARLY]
        w1_rows = w1.rearrange("(p j) f -> p j f", j=LANES)
        sn_sb = sb.tile([P, SIZE], F32, name="sn_sb")
        nc.sync.dma_start(out=dy_raw[:], in_=dyT.rearrange("(p j) x -> p j x", j=LANES))
        w2_rows = w2.rearrange("(p j) d -> p j d", j=LANES)
        nc.sync.dma_start(out=w2_raw[0][:], in_=w2_rows[:, :, 0:HALF])
        nc.sync.dma_start(offsets[:], offs)
        nc.sync.dma_start(out=w2_raw[1][:], in_=w2_rows[:, :, HALF:])
        nc.sync.dma_start(out=w1_early[:], in_=w1_rows[:, :, SIZE - W1_EARLY :])
        nc.sync.dma_start(out=sn_sb[:], in_=sn)
        cs_cols = sb.tile([P, CHUNKS], F32, name="cs_cols")
        with nc.allow_non_contiguous_dma(reason="one factor a partition"):
            nc.sync.dma_start(out=cs_cols[:], in_=cs[0, :].rearrange("(c p) -> p c", p=P))
        nc.sync.dma_start(out=w1_raw[:], in_=w1_rows[:, :, 0 : SIZE - W1_EARLY])

        dy_codes = sb.tile([P, SIZE], U32, name="dy_codes", align_bytes=64)
        dy_scales = sb.tile([P, SIZE], U8, name="dy_scales", align_bytes=64)
        dy_bf = sb.tile([P, SIZE, LANES], BF16, name="dy_bf", align_bytes=64)
        interleave(nc.vector.tensor_copy, dy_bf[:, 0:FIRST, :], dy_raw[:, :, 0:FIRST], 4)
        interleave(nc.vector.tensor_copy, dy_bf[:, FIRST:DY_SPLIT, :], dy_raw[:, :, FIRST:DY_SPLIT], 4)
        interleave(scalar_cast, dy_bf[:, DY_SPLIT:, :], dy_raw[:, :, DY_SPLIT:], 4)
        for h in range(2):
            cols = slice(h * HALF, (h + 1) * HALF)
            quantize(dy_codes[:, cols], dy_scales[:, cols], dy_bf[:, cols, :].rearrange("p x t -> p (x t)"), E5M2)

        w2_codes = sb.tile([P, SIZE], U32, name="w2_codes", align_bytes=64)
        w2_scales = sb.tile([P, SIZE], U8, name="w2_scales", align_bytes=64)
        w2_quads = [w2_raw[h][:].rearrange("p j (i t) -> p i j t", t=LANES) for h in range(2)]
        w2_first = [sb.tile([P, P, LANES], BF16, name="w2_first%d" % h, align_bytes=64) for h in range(2)]
        w2_last = sb.tile([P, 2, P, LANES], BF16, name="w2_last", align_bytes=64)
        last_dealt = w2_last[:].rearrange("p t (h i) j -> p h i j t", h=2)

        def quantize_w2(g, words):
            quantize(w2_codes[:, block(g)], w2_scales[:, block(g)], words.rearrange("p m j -> p (m j)"), E4M3)

        def shared(dst, src, n):
            if n > 0:
                nc.vector.tensor_copy(out=dst[:, 0:n], in_=src[:, 0:n])
            if n < P // 2:
                nc.scalar.copy(out=dst[:, n:], in_=src[:, n:])

        for h in range(2):
            first_dealt = w2_first[h][:].rearrange("p (t i) j -> p i j t", t=2)
            shared(first_dealt, w2_quads[h][:, :, :, 0:2], (W2_SPLIT, P // 2)[h])
            shared(last_dealt[:, h], w2_quads[h][:, :, :, 2:], (0, P // 4)[h])
            quantize_w2(h, w2_first[h][:])
        for t in range(2):
            quantize_w2(2 + t, w2_last[:, t])
        w1_bf = sb.tile([P, LANES, P + PAD, LANES], BF16, name="w1_bf", tag="late", align_bytes=64)[:, :, 0:P, :]
        w1_dealt = w1_bf[:].rearrange("p t r j -> p r j t")
        late_words = (SIZE - W1_EARLY) // LANES
        nc.vector.tensor_copy(out=w1_dealt[:, late_words:], in_=w1_early[:].rearrange("p j (r t) -> p r j t", t=LANES))

        partner = sb.tile([P, LANES, SIZE + PAD], F32, name="partner", tag="partner", align_bytes=64)[:, :, 0:SIZE]
        uT_ps = [bank(LANES + c, "uT_ps%d" % c) for c in range(CHUNKS)]
        for t in range(LANES):
            u_ps = bank(t, "u_ps%d" % t)
            product(u_ps, w2_codes[:, block(t)], w2_scales[:, block(t)], dy_codes, dy_scales)
            nc.scalar.copy(out=u_sb[t][:, 0:SIZE], in_=u_ps[:])

        moved = [sb.tile([P, SIZE], F32, name="moved%d" % h) for h in range(2)]
        halves = (slice(0, P // 2), slice(P // 2, P))
        for t in range(LANES):
            pieces = {1: ((0, HALF), (HALF, SIZE)), LANES - 1: ((0, P), (P, SIZE))}.get(t, ((0, SIZE),))
            for x0, x1 in pieces:
                looked_up = u_sb[t][:].indirect(offsets[:, x0 // BAND : x1 // BAND])
                target = moved[t][:, x0:x1] if t < 2 else partner[:, t, x0:x1]
                nc.vector.tensor_tensor(target, looked_up, sn_sb[:, x0:x1], MULT)
                if t < 2:
                    for lane in range(2):
                        nc.sync.dma_start(out=partner[halves[t], lane, x0:x1], in_=moved[t][halves[lane], x0:x1])

        others = tuple(c for c in range(CHUNKS) if c != POOL_CHUNK)
        own_order = (POOL_CHUNK,) + others
        own_ps = [None] * CHUNKS
        for c in own_order:
            for t in range(LANES):
                if t < 2:
                    turned = uT_ps[c][:].rearrange("p (t h i) -> p h t i", t=LANES, h=2)[:, t, 0:2, :]
                else:
                    turned = uT_ps[c][:, block(t)]
                nc.tensor.transpose(turned, u_sb[t][:, block(c)], identity[:])
        own_pool = sb.tile([P, POOL_COLS, LANES], F32, name="own_pool")
        for c in own_order:
            if c == own_order[-1]:
                by_column = own_ps[POOL_CHUNK][:].rearrange("p (t x) -> p x t", t=LANES)
                nc.scalar.copy(out=own_pool[:], in_=by_column[:, P - POOL_COLS :, :])
            ownT = sb.tile([P, SIZE], F32, name="ownT%d" % c, tag="ownT%d" % c, align_bytes=64)
            nc.scalar.activation(ownT[:], uT_ps[c][:], COPY, scale=cs_cols[:, c : c + 1])
            own_ps[c] = bank(c, "own_ps%d" % c)
            for t in range(LANES):
                nc.tensor.transpose(own_ps[c][:, block(t)], ownT[:, block(t)], identity[:])

        w1_scales = sb.tile([P, SIZE], U8, name="w1_scales", align_bytes=64)
        w1_quads = w1_raw[:].rearrange("p j (r t) -> p r j t", t=LANES)
        for r0 in range(0, late_words, W1_PIECE):
            nc.scalar.copy(out=w1_dealt[:, r0 : r0 + W1_PIECE], in_=w1_quads[:, r0 : r0 + W1_PIECE])

        v_codes = sb.tile([P, SIZE], U32, name="v_codes", align_bytes=64)
        v_scales = sb.tile([P, SIZE], U8, name="v_scales", align_bytes=64)
        v_bf = [sb.tile([P, P, LANES], BF16, name="v_bf%d" % c, tag="v_bf%d" % c, align_bytes=64) for c in range(CHUNKS)]

        def mix(c, n):
            nc.vector.tensor_tensor(
                v_bf[c][:, 0:n, :].rearrange("p (c i) t -> p c t i", i=2),
                own_ps[c][:].rearrange("p (t x) -> p t x", t=LANES)[:, :, 0:n].rearrange("p t (c i) -> p c t i", i=2),
                partner[:, :, c * P : c * P + n].rearrange("p t (c i) -> p c t i", i=2),
                SUBTRACT,
            )

        def quantize_v(c):
            quantize(v_codes[:, block(c)], v_scales[:, block(c)], v_bf[c][:].rearrange("p x t -> p (x t)"), E5M2)

        def quantize_w1(t, tag):
            codes = sb.tile([P, P], U32, name="w1_codes%d" % t, tag=tag, align_bytes=64)
            quantize(codes[:], w1_scales[:, block(t)], w1_bf[:, t, :, :].rearrange("p r j -> p (r j)"), E4M3)
            return codes

        nc.gpsimd.tensor_tensor(
            v_bf[POOL_CHUNK][:, P - POOL_COLS :, :],
            own_pool[:],
            partner[:, :, (POOL_CHUNK + 1) * P - POOL_COLS : (POOL_CHUNK + 1) * P].rearrange("p t x -> p x t"),
            SUBTRACT,
        )
        mix(0, P)
        mix(POOL_CHUNK, P - POOL_COLS)
        for c in others[1:]:
            mix(c, P)

        warm = bank(POOL_CHUNK, "warm")
        for t in range(WARM_UPS):
            product(warm, w2_codes[:, block(t)], w2_scales[:, block(t)], dy_codes, dy_scales)

        for c in others:
            quantize_v(c)
        w1_codes = [quantize_w1(0, "v_bf%d" % others[1])]
        quantize_v(POOL_CHUNK)
        for t, tag in ((1, "v_bf%d" % others[2]), (2, "partner"), (3, "v_bf%d" % POOL_CHUNK)):
            w1_codes.append(quantize_w1(t, tag))

        res = sb.tile([P, LANES, SIZE], F32, name="res", tag="late", align_bytes=64)
        out_rows = out_0.rearrange("(p t) x -> p t x", t=LANES)
        for t in range(LANES):
            acc = bank(LANES + t, "acc%d" % t)
            product(acc, w1_codes[t][:], w1_scales[:, block(t)], v_codes, v_scales)
            copy = nc.vector.tensor_copy if t % 2 == 0 else nc.scalar.copy
            pieces = {0: ((0, HALF), (HALF, SIZE)), LANES - 1: ((0, FIRST), (FIRST, SIZE))}.get(t, ((0, SIZE),))
            for x0, x1 in pieces:
                copy(out=res[:, t, x0:x1], in_=acc[:, x0:x1])
                if t == 0:
                    nc.sync.dma_start(out=out_rows[:, t, x0:x1], in_=res[:, t, x0:x1])
            if t == 1:
                nc.sync.dma_start(out=out_rows[:, 1:2, :], in_=res[:, 1:2, :])
            if t == LANES - 1:
                nc.sync.dma_start(out=out_rows[:, 2:, :], in_=res[:, 2:, :])

        res_codes = sb.tile([P, SIZE], U32, name="res_codes", align_bytes=64)
        res_scales = sb.tile([P, SIZE], U8, name="res_scales", align_bytes=64)
        res_bf = sb.tile([P, SIZE, LANES], BF16, name="res_bf", align_bytes=64)
        out_words = out_1[0].rearrange("p x l -> p (x l)").bitcast(I32)
        split = HALF + RES_SPLIT
        interleave(nc.vector.tensor_copy, res_bf[:, 0:FIRST, :], res[:, :, 0:FIRST], 2)
        interleave(nc.vector.tensor_copy, res_bf[:, FIRST:split, :], res[:, :, FIRST:split], 2)
        interleave(nc.scalar.copy, res_bf[:, split:, :], res[:, :, split:SIZE], 2)
        for h in range(2):
            cols = slice(h * HALF, (h + 1) * HALF)
            quantize(res_codes[:, cols], res_scales[:, cols], res_bf[:, cols, :].rearrange("p x t -> p (x t)"), E4M3)
            nc.sync.dma_start(out=out_words[:, cols], in_=res_codes[:, cols].bitcast(I32))
        for quad in range(4):
            queue = nc.sync if quad % 2 == 0 else nc.scalar
            queue.dma_start(
                out=out_2[0, 4 * quad : 4 * quad + 4, :].bitcast(I32),
                in_=res_scales[32 * quad : 32 * quad + 4, :].bitcast(I32),
            )
